import numpy as np, ml_dtypes
CORES = [1,5,17,21,33,37,49,53]
N = 8
BF = ml_dtypes.bfloat16
def gentries(a):
    return np.ascontiguousarray(a.reshape(8, 16, -1).transpose(0, 2, 1)).reshape(8, -1)
def gtable(e):
    e = np.asarray(e); return np.ascontiguousarray(e.reshape(8, -1, 16).transpose(0, 2, 1)).reshape(128, -1).astype(np.int32)
P, L, S, F, RO = 4096, 2048, 4, 512, 3
H = P - F
def depths(rng, up, top):
    s = np.where(rng.random((N, 8, P)) < up, 1, 1 - rng.geometric(0.5, (N, 8, P))); d = np.zeros((N, 8, P), np.int64); now = np.zeros((N, 8), np.int64)
    for v in range(1, P):
        now = np.minimum(np.maximum(now + s[:, :, v], 0), top); d[:, :, v] = now
    return d
def closed(d):
    e = np.zeros(d.shape, np.int64); last = np.full(d.shape[:-1] + (1,), P, np.int64)
    for k in range(int(np.max(d)) + 1):
        m = np.minimum.accumulate(np.where(d <= k, np.arange(P), P)[..., ::-1], axis=-1)[..., ::-1]
        e = np.where(d == k, np.concatenate([m[..., 1:], last], axis=-1), e)
    return e
def parts(rng):
    up = rng.choice(np.array([0.4, 0.5, 0.6]), (N, 8, 1)); top = rng.integers(3, 13, (N, 8))
    full = np.arange(P) < (P * rng.choice(np.array([8, 12, 14, 16]), (N, 8, 1))) // 16
    d = np.where(full, depths(rng, up, top), 0)
    x = np.where(rng.random((N, 8, 16, P)) < 0.25, rng.integers(0, 4, (N, 8, 16, P)), rng.integers(0, 256, (N, 8, 16, P))) * full[:, :, None, :]
    return x, d, rng.integers(0, 256, (N, 8, 16, L)), rng.integers(0, P, (N, 8, RO, L))
def pack(x, e, w, st):
    return {"x": np.ascontiguousarray(x.reshape(N, 128, P)).astype(np.float32).astype(BF), "w": np.ascontiguousarray(w.reshape(N, 128, L)).astype(np.float32).astype(BF),
            "ends": np.ascontiguousarray(e).astype(np.int32), "start": np.stack([gtable(a.reshape(8, -1)) for a in st])}
def setup_inputs(rng):
    x, d, w, st = parts(rng)
    return pack(x, closed(d), w, st)
def setup_inputs_room(rng):
    x, d, w, st = parts(rng); x = rng.integers(0, 256, x.shape); Q = P // 16; z = F // 4
    at = ((H - z, H), (H - z + 1, H + 1), (H, H + z), (H - 1, H - 1 + z), (P - z, P), (P - z + 1, P + 1), (P - 1, P - 1 + z), (H - z, -1))
    for q in range(N):
        for g in range(8):
            n = int(rng.integers(Q // 2, Q + 1)); a, b = at[(g + q) % 8]; a = a - n; b = P if b < 0 else b - n; D = d[q, g].copy()
            d[q, g] = np.concatenate([np.tile(np.arange(3), Q), D[:a - 3 * Q], np.zeros(1, np.int64), 1 + D[:b - a - 1], D[:P - b]])
            hot = 3 * rng.permutation(Q)[:n]
            st[q, g, 0] = rng.permutation(np.concatenate([hot, rng.choice(hot, L - n)]))
    return pack(x, closed(d), w, st)
def setup_inputs_ties(rng):
    x, d, w, st = parts(rng); lo = rng.choice(np.array([0, 100, 252]), (N, 8, 1, 1))
    x = lo + rng.integers(0, 4, x.shape); x[:, 1::2] = (lo + 2 * rng.integers(0, 2, (N, 8, 1, P)))[:, 1::2]
    return pack(x, closed(d), np.minimum(lo + rng.integers(0, 5, w.shape), 255), st)
def setup_inputs_alike(rng):
    x, d, w, st = parts(rng); x = rng.integers(0, 256, x.shape); e = closed(d); at = np.arange(P)
    names = rng.integers(0, P, (N, 8, RO, 6)); names[..., 0] = 0; names[..., 1] = P - 1
    st = np.take_along_axis(names, rng.integers(0, 6, st.shape), 3)
    for q in range(N):
        g = (np.arange(4) + q) % 8
        e[q, g[0]] = P; st[q, g[0], 0] = rng.choice(np.array([0, P - 1, P - 2, P - 3, P - 1 - S, P - 2 - S]), L)
        e[q, g[1]] = at + 1; e[q, g[1], :2] = P; st[q, g[1], 0] = 0
        e[q, g[2]] = at + 1
        e[q, g[3]] = np.where(at % 2 == 0, P, at + 1); st[q, g[3], 0] = rng.integers(0, P, L)
    return pack(x, e, w, st)
def setup_inputs_far(rng):
    x, d, w, st = parts(rng); x = rng.integers(0, 256, x.shape); w = rng.integers(1, 256, w.shape); g = rng.permutation(8); odd = np.arange(N) % 2 == 1; i4 = np.arange(16)[:, None] % 4
    kid = np.where(odd, rng.integers(3 * P // 4 + 2, P - 1, N), P - 1); low = np.where(odd, rng.integers(3 * P // 4, H, N), P - 1)
    left = np.where(odd, rng.integers(15 * P // 32, P // 2 - 4, N), rng.integers(7 * P // 16 + 1, 15 * P // 32, N)); T = min(P // 7, L // 4)
    st[:, g[:4]] = P - 1
    for q in range(N):
        D = d[q].copy(); b = int(kid[q]); z = int(low[q]); s = int(left[q]); m = D[g[0]]
        d[q, g[0]] = np.concatenate([np.array([0, 1, 2, 3]), 3 + m[:b - 4], np.array([2]), m[:P - b - 1]])
        x[q, g[0], :, b] = 0; st[q, g[0], 0] = 0
        d[q, g[1]] = np.concatenate([np.zeros(z + 1, np.int64), D[g[1]][:P - z - 1]])
        v = rng.choice(np.array([0, z - 2]), L); v[0] = 0; v[1] = z - 2; st[q, g[1], 0] = v
        m = D[g[2]]; d[q, g[2]] = np.concatenate([np.arange(3), 2 + m[:s - 1], m[:P - s - 2]]); st[q, g[2], 0] = 0
        m = D[g[3]]; a = H - 4 + q % 2
        d[q, g[3]] = np.concatenate([m[:H - 4], np.array([0, 0, 1, 2, 3]) if q % 2 else np.array([0, 1, 2, 3, 3]), m[:P - H - 1]])
        v = np.where(rng.random(L) < 0.5, a, rng.integers(H, P, L)); v[0] = a; st[q, g[3], 1] = v
        d[q, g[4]] = np.concatenate([np.tile(np.array([0, 1, 2, 2, 1, 2, 2]), T), D[g[4]][:P - 7 * T]])
        few = np.array([4, 0, 2, 3, 1, 2, 3])[np.arange(P) % 7]
        x[q, g[4]] = np.where(i4 == few, rng.integers(0, 61, (16, P)), rng.integers(200, 256, (16, P)))
        j = rng.permutation(np.concatenate([np.arange(4 * T), rng.integers(0, 4 * T, L - 4 * T)])); st[q, g[4], 0] = 7 * (j // 4)
        w[q, g[4]] = np.where((i4 == (j % 4) // 2) | (i4 == 2 + j % 2), rng.integers(100, 201, (16, L)), 0)
    x[:, g[0], :, 2] = 255; x[:, g[0], :, 3] = 0; x[:, g[0], :, 4] = 255; x[:, g[3], :, H - 1] = 255; x[:, g[3], :, H] = 0
    for k in (1, 2):
        x[:, g[k], :, 2] = 0; x[:, g[k], :, 3] = 255
    e = closed(d)
    for q in range(N):
        z = int(low[q]); e[q, g[1], :z + 1] = z + 1; e[q, g[1], 2] = 3
    return pack(x, e, w, st)
def setup_inputs_spread(rng):
    x, d, w, st = parts(rng)
    d = depths(rng, 0.35 + 0.35 * rng.random((N, 8, 1)), np.exp2(1 + 5 * rng.random((N, 8))).astype(np.int64) + 1)
    x = np.minimum((np.exp2(8 * rng.random((N, 8, 1, P))) * rng.random((N, 8, 16, P))).astype(np.int64), 255)
    w = np.minimum((np.exp2(8 * rng.random((N, 8, 1, L))) * rng.random((N, 8, 16, L))).astype(np.int64), 255)
    st = np.minimum((P * rng.random((N, 8, RO, L)) ** rng.choice(np.array([1, 2, 4]), (N, 8, 1, 1))).astype(np.int64), P - 1)
    return pack(x, closed(d), w, st)
def check_inputs(d):
    bad = []
    for k in ("x", "w"):
        v = d[k].astype(np.float32)
        if not np.all((v >= 0) & (v <= 255) & (v == np.floor(v))): bad.append("whole numbers from 0 to 255 in " + k)
    e = d["ends"].astype(np.int64); n = e - np.arange(P)
    if np.min(n) < 1 or np.max(e) > P: bad.append("range of ends")
    else:
        big = e; most = np.zeros(e.shape, np.int64); k = 1
        while k <= P:
            sel = (n >= k) & (n < 2 * k)
            most = np.where(sel, np.maximum(big, np.take_along_axis(big, np.where(sel, e - k, 0), 2)), most)
            big = np.concatenate([np.maximum(big[..., :P - k], big[..., k:]), big[..., P - k:]], axis=2); k = 2 * k
        if np.any(most > e): bad.append("runs that cross")
    if np.min(d["start"]) < 0 or np.max(d["start"]) > P - 1: bad.append("range of start")
    return bad
def grow(x, e, w, v):
    G = np.arange(8)[:, None]; at = np.arange(P); n = np.zeros((8, L), np.int64); par = v
    for i in range(S):
        ev = e[G, v]; a = np.minimum(v + 1, P - 1); b = e[G, a]; kids = ev > v + 1; two = kids & (b < ev); b = np.minimum(b, P - 1)
        ra = np.add.reduce(np.maximum(w - x[G, a], 0), axis=2); rb = np.add.reduce(np.maximum(w - x[G, b], 0), axis=2)
        par = np.where(kids, v, par); n = n + kids; v = np.where(kids, np.where(two & (rb > ra), b, a), v)
    hit = (n >= 2) & (e[G, v] == v + 1); gi = np.broadcast_to(G, v.shape)[hit]
    head = np.zeros((8, P), bool); head[gi, v[hit]] = True; mark = np.zeros((8, P), bool); mark[gi, par[hit]] = True
    zero = np.zeros((8, 1), np.int64); reach = np.maximum.accumulate(np.where(mark, e, 0), axis=1)
    top = mark & (np.concatenate([zero, reach[:, :-1]], axis=1) <= at); inside = reach > at; keep = ~head
    first = np.maximum.accumulate(np.where(top, at, 0), axis=1)
    K = np.concatenate([zero, np.add.accumulate(keep.astype(np.int64), axis=1)], axis=1)
    M = np.concatenate([zero, np.add.accumulate(keep * (1 + 2 * inside), axis=1)], axis=1)
    size = np.where(inside, K[G, e] - K[:, :P], M[G, e] - M[:, :P]); s = K[G, e[G, first]] - K[G, first]
    nx = np.zeros((8, P, 16), np.int64); ne = np.zeros((8, P), np.int64) + at + 1
    for c in range(3):
        q = np.where(inside, M[G, first] + c * s + K[:, :P] - K[G, first], M[:, :P])
        gk, vk = np.nonzero(keep & (inside | (c == 0)) & (q < P)); qk = q[gk, vk]
        nx[gk, qk] = np.maximum(x[gk, vk] - c, 0); ne[gk, qk] = qk + size[gk, vk]
    return nx, ne
def reference(x, w, ends, start):
    X = np.ascontiguousarray(x.astype(np.float32).astype(np.int64).reshape(N, 8, 16, P).transpose(0, 1, 3, 2)); E = ends.astype(np.int64)
    W = np.ascontiguousarray(w.astype(np.float32).astype(np.int64).reshape(N, 8, 16, L).transpose(0, 1, 3, 2))
    st = np.stack([gentries(a) for a in start]).astype(np.int64).reshape(N, 8, RO, L)
    for t in range(RO):
        both = [grow(X[r], E[r], W[r], st[r, :, t]) for r in range(N)]
        gx = np.stack([a for a, b in both]); ge = np.stack([b for a, b in both])
        X = np.concatenate([gx[:, :, :H], np.roll(gx[:, :, H:], 1, axis=0)], axis=2)
        E = np.concatenate([np.minimum(ge[:, :, :H], H), np.roll(np.minimum(ge[:, :, H:], P), 1, axis=0)], axis=2)
    return {"y": np.ascontiguousarray(X.transpose(0, 1, 3, 2)).reshape(N, 128, P).astype(np.float32).astype(BF), "ye": E.astype(np.float32)}

@@ -1,0 +1,654 @@
+import numpy as np
+from concourse.bass import DstId, RemoteDMATransfer
+from concourse.mybir import dt, AluOpType, AxisListType, ActivationFunctionType
+import comms_topo
+
+RO = 3
+NLO = 20
+
+SCRATCH = {
+    "BIG": ("sbuf", [128, 20736], "bfloat16"),
+    "VPAY": ("sbuf", [128, 4096], "bfloat16"),
+    "WP": ("sbuf", [128, 2048], "bfloat16"),
+    "INFO": ("sbuf", [128, 4112], "bfloat16"),
+    "GH": ("sbuf", [128, 4128], "bfloat16"),
+    "GV": ("sbuf", [128, 4096], "bfloat16"),
+    "G1": ("sbuf", [128, 4112], "bfloat16"),
+    "VLS": ("sbuf", [128, 4096], "bfloat16"),
+    "SZB": ("sbuf", [128, 3584], "bfloat16"),
+    "XS": ("sbuf", [128, 512], "bfloat16"),
+    "SZS": ("sbuf", [128, 512], "bfloat16"),
+    "HB": ("sbuf", [128, 256], "bfloat16"),
+    "STI": ("sbuf", [128, 384], "int32"),
+    "EI": ("sbuf", [128, 256], "int32"),
+    "AL": ("sbuf", [128, 128], "uint16"),
+    "BL": ("sbuf", [128, 128], "uint16"),
+    "EL": ("sbuf", [128, 264], "uint16"),
+    "OFF": ("sbuf", [128, 256], "uint16"),
+    "VLL": ("sbuf", [128, 256], "uint16"),
+    "QL": ("sbuf", [128, 256], "uint16"),
+    "XL": ("sbuf", [128, 256], "uint16"),
+    "PI": ("sbuf", [128, 4], "int32"),
+    "COL": ("sbuf", [128, 32], "float32"),
+    "ROW": ("sbuf", [128, 160], "float32"),
+    "ROW2": ("sbuf", [128, 160], "float32"),
+    "RC": ("sbuf", [128, 8], "float32"),
+}
+for _t in range(RO + 1):
+    SCRATCH["X%d" % _t] = ("sbuf", [128, 4112], "bfloat16")
+for _t in range(RO):
+    SCRATCH["LZ%d" % _t] = ("sbuf", [128, 512], "bfloat16")
+for _n in ("LP", "LN", "LB", "L1", "L2", "L3", "L4", "LV", "SELH"):
+    SCRATCH[_n] = ("sbuf", [128, 2048], "bfloat16")
+for _n in ("ID", "TRI", "TRI2", "SHF", "ONE", "CODE", "MISS", "NV", "MM", "DD", "GQ", "AF0", "AF1"):
+    SCRATCH[_n] = ("sbuf", [128, 128], "float32")
+for _n in ("PKI", "PPI", "PSI"):
+    SCRATCH[_n] = ("sbuf", [128, 256], "int32")
+for _n in ("TI", "THI", "TLO"):
+    SCRATCH[_n] = ("sbuf", [128, 128], "int32")
+for _n in ("HIb", "LOb"):
+    SCRATCH[_n] = ("sbuf", [128, 128], "bfloat16")
+for _n in ("VG", "VC", "REM", "QW", "ZERO", "KD", "TW", "TWE", "HF", "EG", "HK", "HINC", "A1", "KB", "VGK",
+           "OX", "OUT", "KI", "POS", "S2", "T1", "T2", "T3", "T4", "T5", "T6"):
+    SCRATCH[_n] = ("sbuf", [128, 256], "float32")
+for _n in ("SZ", "HM", "HME", "RS", "J2", "EF"):
+    SCRATCH[_n] = ("sbuf", [128, 264], "float32")
+for _n in ("B0", "B1", "H0", "H1", "HMb", "J0", "J1", "P0", "P1", "S20", "S21", "Z0", "Z1"):
+    SCRATCH[_n] = ("sbuf", [128, 256], "bfloat16")
+for _n in range(8):
+    SCRATCH["b%d" % _n] = ("psum", [128, 512], "float32")
+
+SEMAPHORES = (["sV", "sS", "sP", "sG"] + ["d%d" % _k for _k in range(72)]
+              + ["%s%d" % (_a, _k) for _a in ("rx", "rz", "lx", "lz") for _k in range(RO)])
+
+ALL = (0, 128, 1)
+ONEROW = (0, 1, 1)
+ACT = ActivationFunctionType
+OP = AluOpType
+
+
+def v(name, c0=0, c1=None, cs=1, p=ALL):
+    if c1 is None:
+        c1 = 4096 if name in ("y", "ye", "x", "ends") else SCRATCH[name][1][1]
+    return (name, p, c0, c1, cs)
+
+
+BO = 4096
+
+
+def bg(c0, c1, cs=1):
+    return v("BIG", BO + c0, BO + c1, cs)
+
+
+def ind(win, off):
+    return ("@", win, off)
+
+
+def pmask(p):
+    m = 0
+    for k in range(p[0], p[1], p[2]):
+        m |= 1 << k
+    return m
+
+
+def rank_program(g, core, T, topo):
+    rank = T.rank_of(core)
+    if rank is None:
+        return
+    ops = []
+    masks = {}
+
+    def pm(p):
+        if p not in masks:
+            masks[p] = pmask(p)
+        return masks[p]
+
+    def flat(x, out):
+        if isinstance(x, tuple):
+            if x[0] == "@":
+                out.append(x[1])
+                out.append(x[2])
+            elif len(x) == 5:
+                out.append(x)
+        return out
+
+    def add(q, reads, writes, call, sem=None, n=1):
+        rd = []
+        for x in reads:
+            flat(x, rd)
+        wr = []
+        for x in writes:
+            if x[0] == "@":
+                wr.append(x[1])
+                rd.append(x[2])
+            else:
+                wr.append(x)
+        ops.append({"q": q, "r": rd, "w": wr, "call": call, "sem": sem, "n": n})
+
+    def ap(x):
+        if not isinstance(x, tuple):
+            return x
+        if x[0] == "@":
+            return ap(x[1]).indirect(ap(x[2]))
+        name, p, c0, c1, cs = x
+        return T[name][p[0]:p[1]:p[2], c0:c1:cs] if (p[2] != 1 or cs != 1) else T[name][p[0]:p[1], c0:c1]
+
+    def copy(out, i):
+        add("V", [i], [out], lambda: g.vector.tensor_copy(ap(out), ap(i)))
+
+    def tt(out, a, b, op):
+        add("V", [a, b], [out], lambda: g.vector.tensor_tensor(ap(out), ap(a), ap(b), op))
+
+    def ts(out, a, s1, op0, s2=None, op1=None):
+        if op1 is None:
+            add("V", [a, s1], [out], lambda: g.vector.tensor_scalar(ap(out), ap(a), ap(s1), None, op0))
+        else:
+            add("V", [a, s1, s2], [out], lambda: g.vector.tensor_scalar(ap(out), ap(a), ap(s1), ap(s2), op0, op1))
+
+    def red(out, i, op):
+        add("V", [i], [out], lambda: g.vector.tensor_reduce(ap(out), ap(i), AxisListType.X, op))
+
+    def scan(out, d0, d1, init, op0, op1):
+        add("V", [d0, d1, init], [out], lambda: g.vector.tensor_tensor_scan(ap(out), ap(d0), ap(d1), ap(init), op0, op1))
+
+    def fill(out, c):
+        add("V", [], [out], lambda: g.vector.memset(ap(out), c))
+
+    def act(out, i, func, bias=None, scale=None):
+        def call():
+            kw = {}
+            if bias is not None:
+                kw["bias"] = bias
+            if scale is not None:
+                kw["scale"] = ap(scale)
+            return g.scalar.activation(ap(out), ap(i), func, **kw)
+        add("S", [i, scale], [out], call)
+
+    def mm(out, l, r, start, stop):
+        add("P", [l, r], [out], lambda: g.tensor.matmul(ap(out), ap(l), ap(r), start, stop))
+
+    def tr(out, i, idn):
+        add("P", [i, idn], [out], lambda: g.tensor.transpose(ap(out), ap(i), ap(idn)))
+
+    def iota(out, pattern, base, cm, small=True):
+        if small:
+            add("G", [], [out], lambda: g.iota(ap(out), pattern, base, cm, allow_small_or_imprecise_dtypes=True))
+        else:
+            add("G", [], [out], lambda: g.iota(ap(out), pattern, base, cm))
+
+    def asel(out, i, pattern, cop, fillv, base, cm):
+        add("G", [i], [out], lambda: g.affine_select(ap(out), ap(i), pattern, cop, fillv, base, cm))
+
+    nd = [0]
+
+    def dma(out, i):
+        sem = "d%d" % nd[0]
+        nd[0] += 1
+        add("Y", [i], [out], lambda: g.sync.dma_start(ap(out), ap(i)), sem, 16)
+
+    def rows(name, r, c0, src):
+        dma(v(name, c0, c0 + 4096, 1, (r, 128, 16)), v(src))
+
+    def bwd(out, lname, src, c0, k, first=True, last=True):
+        for i in range(16):
+            mm(out, v(lname, 128 * i, 128 * i + 128), v(src, c0 + i, c0 + 16 * k, 16), first and i == 0, last and i == 15)
+
+    dma(v("EI"), v("ends", 0, 4096, 1, (0, 8, 1)))
+    dma(v("STI"), v("start", 0, 384))
+    dma(v("X0", 0, 4096), v("x"))
+    dma(v("WP"), v("w", 0, 2048))
+    PIc = v("PI", 0, 1)
+
+    def col(k):
+        return v("COL", k, k + 1)
+    iota(PIc, [[0, 1]], 0, 1, False)
+    iota(v("VG"), [[1, 256]], 0, 256)
+    iota(bg(0, 2048), [[-1, 16], [1, 128]], 0, 0)
+    fill(v("ONE"), 1.0)
+    fill(v("INFO"), 0.0)
+    asel(v("SHF"), v("ONE"), [[-1, 128]], OP.is_equal, 0.0, -1, 1)
+    asel(v("ID"), v("ONE"), [[-1, 128]], OP.is_equal, 0.0, 0, 1)
+    ts(v("PI", 1, 2), PIc, 4, OP.arith_shift_right)
+    ts(v("PI", 2, 3), PIc, 15, OP.bitwise_and)
+    G16, GB, II, GB2 = col(0), col(1), col(2), col(3)
+    ts(GB, v("PI", 1, 2), 4096.0, OP.mult)
+    ts(v("VC"), v("VG"), GB, OP.subtract)
+    ts(G16, v("PI", 1, 2), 16.0, OP.mult)
+    ts(GB2, v("PI", 1, 2), 8192.0, OP.mult)
+    copy(II, v("PI", 2, 3))
+    for t in range(RO + 1):
+        fill(v("X%d" % t, 4096, 4112), 0.0)
+    fill(v("ZERO"), 0.0)
+    fill(v("ROW"), 0.0)
+    fill(v("ROW2"), 0.0)
+    SZ = v("SZ", 0, 256)
+    SZ1 = v("SZ", 1, 257)
+
+    def edge(name):
+        mm(v("b6", 0, 1), v("SHF"), v(name, 0, 1), True, True)
+        copy(v(name, 256, 257), v("b6", 0, 1))
+
+    def tables():
+        ts(v("T1"), SZ, -1.0, OP.add)
+        ts(v("KD"), v("T1"), 1.0, OP.min)
+        edge("SZ")
+        tt(v("TW"), SZ1, v("T1"), OP.is_lt)
+        tt(v("T3"), v("KD"), v("VC"), OP.add)
+        tt(v("T2"), v("TW"), SZ1, OP.mult)
+        tt(v("T4"), v("T2"), v("T3"), OP.add)
+        act(v("B0"), v("T4"), ACT.Copy)
+        rows("INFO", 0, 1, "B0")
+        tt(v("B1"), v("T4"), v("B0"), OP.subtract)
+        rows("INFO", 1, 1, "B1")
+
+    def tables2():
+        tt(v("EF", 0, 256), v("VC"), v("T1"), OP.add)
+        mm(v("b6", 0, 1), v("SHF"), v("EF", 0, 1), True, True)
+        tt(v("EG"), v("VG"), SZ, OP.add)
+        ts(v("HF"), v("KD"), -1.0, OP.mult, 1.0, OP.add)
+        tt(v("TWE"), v("TW"), v("EG"), OP.mult)
+
+    tt(SZ, v("EI"), v("VC"), OP.subtract)
+    tables()
+    ts(v("LP"), bg(0, 2048), G16, OP.is_equal)
+
+    def weight(name, k, terms, onv):
+        c = col(k)
+        for n, (row, wgt) in enumerate(terms):
+            if n == 0:
+                ts(c, II, float(row), OP.is_equal, float(wgt), OP.mult)
+            else:
+                ts(col(31), II, float(row), OP.is_equal, float(wgt), OP.mult)
+                tt(c, c, col(31), OP.add)
+        if onv:
+            ts(v(name), v("LP"), c, OP.mult)
+        else:
+            act(v(name), v("LP"), ACT.Copy, None, c)
+    weight("LB", 8, [(0, 1), (1, 1)], True)
+    ts(v("LN"), v("LP"), -1.0, OP.mult)
+    weight("L1", 9, [(0, 1), (1, 1), (2, 8192)], False)
+    weight("L2", 10, [(3, 1), (4, 1)], False)
+    weight("L3", 11, [(0, 4096), (1, 4096), (2, 0.5), (3, 0.5)], False)
+    weight("L4", 13, [(4, 1), (5, 1)], True)
+    weight("LV", 14, [(0, 64), (1, 1)], True)
+    ts(col(4), II, 14.0, OP.is_ge, 512.0, OP.mult)
+    ts(v("REM"), v("VC"), col(4), OP.subtract, -1.0, OP.mult)
+    ts(v("REM"), v("REM"), 3584.0, OP.add)
+    fill(v("SELH"), 1.0)
+    iota(v("TRI"), [[16, 8], [0, 16]], 0, 0)
+    iota(v("QW"), [[16, 256]], 0, 1)
+    ts(v("QW"), v("QW"), G16, OP.subtract)
+    ts(v("TRI"), v("TRI"), G16, OP.is_equal)
+    asel(v("TRI"), v("TRI"), [[1, 128]], OP.is_gt, 0.0, 0, -1)
+    ts(v("TRI2"), v("TRI"), 2.0, OP.mult)
+    asel(v("SELH"), v("SELH"), [[128, 4], [-1, 4], [-4, 128]], OP.is_equal, 0.0, 0, 1)
+    iota(v("GH"), [[0, 4128]], 0, 0)
+    iota(v("BIG", 0, 4096), [[1, 4], [0, 64], [4, 16]], 1, 0)
+    iota(v("VPAY"), [[0, 4], [1, 64], [0, 16]], 1, 0)
+    iota(v("GV"), [[0, 4096]], 0, 0)
+    dma(v("VPAY", 0, 4096, 1, (0, 128, 16)), v("BIG", 0, 4096, 1, (0, 128, 16)))
+
+    IG = (0, 1024)
+    TA = (2048, 3072)
+    RA = (9216, 4096)
+    TB = (5120, 6144)
+    RB = (7168, 8192)
+
+    for t in range(RO):
+        X, XN = "X%d" % t, "X%d" % (t + 1)
+        AFn = ["AF0", "AF1"]
+
+        def w64(name, h):
+            return v(name, 64 * h, 64 * h + 64)
+
+        def big(base, h):
+            return bg(base[h], base[h] + 1024)
+
+        def info(h):
+            act(big(IG, h), ind(v("INFO", 0, 4112), w64("AL", h)), ACT.Copy)
+            bwd(v("b%d" % h, 0, 64), "LB", "BIG", BO + IG[h], 64)
+
+        def first_kid(h):
+            tt(big(TA, h), ind(v(X), w64("AL", h)), v("WP", 1024 * h, 1024 * h + 1024), OP.subtract)
+            act(big(RA, h), big(TA, h), ACT.Relu, None, -1.0)
+
+        def first_sum(h):
+            bwd(v("b%d" % (2 + h), 0, 64), "LN", "BIG", BO + RA[h], 64, True, False)
+
+        def second_kid(h, s):
+            copy(w64("BL", h), v("b%d" % h, 0, 64))
+            tt(big(TB, h), ind(v(X), w64("BL", h)), v("WP", 1024 * h, 1024 * h + 1024), OP.subtract)
+            act(big(RB, h), big(TB, h), ACT.Relu, None, -1.0)
+            bwd(v("b%d" % (2 + h), 0, 64), "LP", "BIG", BO + RB[h], 64, False, True)
+            tt(w64("MM", h), v("b%d" % h, 0, 64), w64(AFn[s % 2], h), OP.min)
+            tt(w64("DD", h), v("b%d" % h, 0, 64), w64("MM", h), OP.subtract)
+
+        def decide(h, s):
+            ts(w64("GQ", h), v("b%d" % (2 + h), 0, 64), 0.0, OP.is_gt)
+            tt(w64("GQ", h), w64("GQ", h), w64("DD", h), OP.mult)
+            tt(w64("NV", h), w64("GQ", h), w64("MM", h), OP.add)
+            if s < 3:
+                ts(w64("AL", h), w64("NV", h), 1.0, OP.add)
+                ts(w64(AFn[(s + 1) % 2], h), w64("NV", h), 1.0, OP.add)
+            if s == 1:
+                tt(w64("MISS", h), w64(AFn[0], h), w64(AFn[1], h), OP.is_le)
+                ts(w64("MISS", h), w64("MISS", h), 8192.0, OP.mult)
+
+        for h in range(2):
+            s0 = v("STI", 128 * t + 64 * h, 128 * t + 64 * h + 64)
+            ts(w64("AL", h), s0, 1.0, OP.add)
+            ts(w64("AF0", h), s0, 1.0, OP.add)
+        info(0)
+        info(1)
+        for s in range(4):
+            first_kid(0)
+            first_sum(0)
+            if s > 0:
+                decide(1, s - 1)
+                info(1)
+            else:
+                first_kid(1)
+                first_sum(1)
+            second_kid(0, s)
+            if s > 0:
+                first_kid(1)
+                first_sum(1)
+            second_kid(1, s)
+            if s == 0:
+                tables2()
+            if s == 1:
+                copy(v("EF", 256, 257), v("b6", 0, 1))
+                copy(v("EL", 0, 257), v("EF", 0, 257))
+                iota(v("BIG", 0, 4096), [[0, 4096]], 0, 0)
+            decide(0, s)
+            if s < 3:
+                info(0)
+        decide(1, 3)
+        tt(v("CODE"), v("NV"), v("MISS"), OP.add)
+        tr(v("b7", 0, 128), v("CODE"), v("ID"))
+        copy(v("TI"), v("b7", 0, 128))
+        ts(v("TLO"), v("TI"), 63, OP.bitwise_and)
+        copy(v("LOb"), v("TLO"))
+        ts(v("THI"), v("TI"), 6, OP.arith_shift_right)
+        copy(v("HIb"), v("THI"))
+        for k in range(64):
+            ts(bg(128 * k, 128 * k + 128), v("HIb"), float(k), OP.is_equal)
+            if NLO + k < 64:
+                n = NLO + k
+                act(bg(8192 + 128 * n, 8192 + 128 * n + 128), v("LOb"), ACT.Sign, 0.5 - n)
+        for n in range(NLO):
+            ts(bg(8192 + 128 * n, 8192 + 128 * n + 128), v("LOb"), float(n), OP.is_equal)
+        fill(bg(16384, 16512), -1.0)
+        for gg in range(8):
+            for i in range(16):
+                c = 16 * gg + i
+                mm(v("b4", gg // 2, 260, 4, (64 * (gg % 2), 64 * (gg % 2) + 64, 1)), bg(c, 8192, 128), bg(8192 + c, 16512, 128), i == 0, i == 15)
+        copy(v("T1"), v("b4", 4, 260))
+        copy(v("HB", 0, 4 * NLO), v("b4", 0, 4 * NLO))
+        tt(v("HB", 4 * NLO, 256), v("b4", 4 * NLO, 256), v("T1", 4 * NLO, 256), OP.subtract)
+        for cc in range(4):
+            for gh in range(4):
+                mm(v("b5", 64 * cc, 64 * cc + 64), v("SELH", 128 * (4 * gh + cc), 128 * (4 * gh + cc) + 128), v("HB", gh, 256, 4), gh == 0, gh == 3)
+        HM = v("HM", 0, 256)
+        tt(HM, v("b5", 0, 256), v("HF"), OP.min)
+        red(v("RC", 0, 1), HM, OP.add)
+        mm(v("b6", 2, 3), v("TRI"), v("RC", 0, 1), True, True)
+        copy(v("HMb"), HM)
+        rows("GH", 2, 15, "HMb")
+        scan(v("HINC"), v("ZERO"), HM, v("b6", 2, 3), OP.add, OP.add)
+        copy(v("H0"), v("HINC"))
+        rows("GH", 0, 16, "H0")
+        tt(v("H1"), v("HINC"), v("H0"), OP.subtract)
+        rows("GH", 1, 16, "H1")
+        edge("HM")
+        tt(v("HK"), v("HM", 1, 257), v("KD"), OP.mult)
+        tt(v("HK"), v("HK"), v("EG"), OP.mult)
+        ts(v("VGK"), HM, 65536.0, OP.mult)
+        tt(v("VGK"), v("VGK"), v("VG"), OP.add)
+        for k in (0, 2, 1, 3):
+            w = 65 if k == 3 else 64
+            o, i = v("G1", 1024 * k, 1024 * k + 16 * w), ind(v("GH", 16, 4112), v("EL", 64 * k, 64 * k + w))
+            if k < 2:
+                copy(o, i)
+            else:
+                act(o, i, ACT.Copy)
+            bwd(v("b7", 64 * k, 64 * k + w), "L1", "G1", 1024 * k, w)
+        ts(v("T2"), v("HINC"), 2.0, OP.mult, 12288.0, OP.add)
+        tt(v("T2"), v("T2"), v("VC"), OP.subtract)
+        tt(v("T2"), v("T2"), HM, OP.mult)
+        tt(v("KB"), v("VC"), v("HINC"), OP.subtract)
+        tt(v("KB"), v("KB"), v("T2"), OP.add)
+        ts(v("HME", 0, 257), v("b7", 0, 257), 8192.0, OP.is_ge)
+        tt(v("T4"), v("TWE"), v("HME", 1, 257), OP.mult)
+        tt(v("T4"), v("T4"), v("HK"), OP.max)
+
+        def maxscan(out, src, rc, ini, fillers):
+            red(v("RC", rc, rc + 1), src, OP.max)
+            tr(v("b6", 128, 256, 1, ONEROW), v("RC", rc, rc + 1), v("ID"))
+            fillers[0]()
+            scan(v("ROW", 1, 129, 1, ONEROW), v("ROW2", 0, 128, 1, ONEROW), v("b6", 128, 256, 1, ONEROW), 0.0, OP.max, OP.max)
+            mm(v("b6", ini, ini + 1), v("ROW", 0, 128, 1, ONEROW), v("ID", 0, 1, 1, ONEROW), True, True)
+            fillers[1]()
+            scan(out, src, src, v("b6", ini, ini + 1), OP.max, OP.max)
+
+        def f1():
+            ts(v("T2"), v("HME", 0, 256), -8192.0, OP.mult)
+
+        def f2():
+            tt(v("T2"), v("T2"), v("b7", 0, 256), OP.add)
+        maxscan(v("RS", 1, 257), v("T4"), 1, 4, (f1, f2))
+        tt(v("KI"), v("RS", 1, 257), v("VGK"), OP.is_gt)
+        red(v("RC", 2, 3), v("KI"), OP.add)
+        mm(v("b6", 6, 7), v("ID"), GB2, True, False)
+        mm(v("b6", 6, 7), v("TRI2"), v("RC", 2, 3), False, True)
+        copy(v("RS", 0, 1), v("b6", 4, 5))
+        tt(v("OX"), v("RS", 0, 256), v("VG"), OP.is_le)
+        scan(v("J2", 1, 257), v("KI"), v("KI"), v("b6", 6, 7), OP.add, OP.add)
+        copy(v("J2", 0, 1), v("b6", 6, 7))
+        act(v("J0"), v("J2", 1, 257), ACT.Copy)
+        rows("GH", 3, 16, "J0")
+        tt(v("T5"), v("J2", 0, 256), v("OX"), OP.mult)
+
+        def f3():
+            tt(v("J1"), v("J2", 1, 257), v("J0"), OP.subtract)
+            rows("GH", 4, 16, "J1")
+
+        def f4():
+            ts(v("KB"), v("KB"), GB2, OP.subtract)
+        maxscan(v("T6"), v("T5"), 3, 8, (f3, f4))
+        tt(v("POS"), v("KB"), v("T6"), OP.add)
+        copy(v("OFF"), v("POS"))
+        act(v("P0"), v("POS"), ACT.Copy)
+        rows("GV", 0, 0, "P0")
+        tt(v("S2"), v("J2", 1, 257), v("T6"), OP.subtract)
+        act(v("S20"), v("S2"), ACT.Copy)
+        rows("GV", 2, 0, "S20")
+        copy(ind(v("BIG", 0, 20480), v("OFF")), v("VPAY"))
+        for k in range(4):
+            act(v("G1", 1024 * k, 1024 * k + 1024), ind(v("GH", 16, 4112), v("EL", 64 * k, 64 * k + 64)), ACT.Copy)
+            bwd(v("b5", 256 + 64 * k, 256 + 64 * k + 64), "L2", "G1", 1024 * k, 64)
+        tt(v("P1"), v("POS"), v("P0"), OP.subtract)
+        rows("GV", 1, 0, "P1")
+        tt(v("S21"), v("S2"), v("S20"), OP.subtract)
+        rows("GV", 3, 0, "S21")
+        ts(bg(0, 2560), v("BIG", 0, 2560), 0.0, OP.is_equal)
+        act(bg(2560, 4096), v("BIG", 2560, 4096), ACT.Relu, 1.0, -1.0)
+        tt(v("A1"), SZ, v("HINC"), OP.add)
+        tt(v("A1"), v("A1"), HM, OP.subtract)
+        tt(v("A1"), v("A1"), v("T2"), OP.subtract)
+        tt(v("OUT"), v("RS", 1, 257), v("VG"), OP.is_le)
+        tt(v("T5"), v("b5", 256, 512), v("J2", 0, 256), OP.subtract)
+        tt(v("T5"), v("T5"), v("OUT"), OP.mult)
+        tt(v("T5"), v("T5"), v("A1"), OP.add)
+        act(v("Z0"), v("T5"), ACT.Copy)
+        rows("GV", 4, 0, "Z0")
+        for k in range(4):
+            a = 1024 * k
+            scan(v("VLS", a, a + 1024), bg(a, a + 1024), v("BIG", a, a + 1024), 0.0 if k == 0 else v("VLS", a - 1, a), OP.mult, OP.add)
+            bwd(v("b%d" % k, 0, 64), "LV", "VLS", a, 64)
+            if k == 0:
+                tt(v("Z1"), v("T5"), v("Z0"), OP.subtract)
+                rows("GV", 5, 0, "Z1")
+        for k in range(4):
+            ts(v("VLL", 64 * k, 64 * k + 64), v("b%d" % k, 0, 64), -65.0, OP.add)
+
+        def gat(k, out, win):
+            i = ind(win, v("VLL", 64 * k, 64 * k + 64))
+            if k < 2:
+                act(out, i, ACT.Copy)
+            else:
+                copy(out, i)
+        for k in (0, 2, 1, 3):
+            a = 1024 * k
+            gat(k, bg(12288 + a, 12288 + a + 1024), v("GV"))
+            bwd(v("b4", 64 * k, 64 * k + 64), "L3", "BIG", BO + 12288 + a, 64)
+        for k in (0, 2, 1, 3):
+            gat(k, bg(1024 * k, 1024 * k + 1024), v(X))
+        act(bg(4096, 6144), bg(0, 2048), ACT.Relu, -1.0)
+        copy(v("PKI"), v("b4", 0, 256))
+        ts(v("PPI"), v("PKI"), 12, OP.arith_shift_right)
+        ts(v("PSI"), v("PKI"), 4095, OP.bitwise_and)
+        tt(v("T1"), v("QW"), v("PPI"), OP.subtract)
+        tt(v("T2"), v("T1"), v("PSI"), OP.is_gt)
+        ts(v("T3"), v("T1"), 0.0, OP.is_gt)
+        tt(v("T3"), v("T3"), v("T2"), OP.add)
+        tt(v("T4"), v("T3"), v("PSI"), OP.mult)
+        tt(v("T4"), v("QW"), v("T4"), OP.subtract)
+        copy(v("QL"), v("T4"))
+        ts(v("T3"), v("T3"), 4096.0, OP.mult)
+        tt(v("T5"), v("T3"), v("T4"), OP.add)
+        copy(v("XL"), v("T5"))
+        act(bg(6144, 8192), bg(2048, 4096), ACT.Relu, -1.0)
+        dst = T.cores[(rank + 1) % len(T.cores)]
+        src = T.cores[(rank - 1) % len(T.cores)]
+
+        def send(name, to, rsem, lsem):
+            rid, pid, _se = topo.addr(dst)
+            add("G", [v(name)], [], lambda: g.remote_dma(ap(to), ap(v(name)), T.sem[rsem], T.sem[lsem], pid, rid, topo.mask(core, dst)),
+                lsem, len(topo.engines(core, dst)))
+            add("R", [], [to], None, rsem, len(topo.engines(src, core)))
+
+        def sizes(out, lo, hi, onv):
+            i = ind(bg(12288, 16384), v("QL", lo // 16, hi // 16))
+            if onv:
+                copy(out, i)
+            else:
+                act(out, i, ACT.Copy)
+
+        def szc(i):
+            s = v("SZB", 256 * i, 256 * i + 256) if i < 14 else v("LZ%d" % t, 256 * (i - 14), 256 * (i - 14) + 256)
+            mm(v("b7", 0, 256), v("L4", 128 * i, 128 * i + 128), s, i == 0, i == 15)
+
+        def xl(lo, hi):
+            return ind(bg(0, 12288), v("XL", lo // 16, hi // 16))
+        sizes(v("SZS"), 3584, 4096, False)
+        send("SZS", v("LZ%d" % t), "rz%d" % t, "lz%d" % t)
+        for k in (0, 3, 1, 4, 2, 5, 6):
+            sizes(v("SZB", 512 * k, 512 * k + 512), 512 * k, 512 * k + 512, k < 3)
+            szc(2 * k)
+            szc(2 * k + 1)
+        szc(14)
+        szc(15)
+        ts(bg(8192, 12288), bg(0, 4096), 2.0, OP.subtract, 0.0, OP.max)
+        copy(v("XS"), xl(3584, 4096))
+        send("XS", v(XN, 3584, 4096), "rx%d" % t, "lx%d" % t)
+        if t < RO - 1:
+            act(v(XN, 1024, 3584), xl(1024, 3584), ACT.Copy)
+            tt(SZ, v("b7", 0, 256), v("REM"), OP.min)
+            tables()
+            copy(v(XN, 0, 1024), xl(0, 1024))
+        else:
+            copy(v(XN, 0, 1024), xl(0, 1024))
+            dma(v("y", 0, 1024), v(XN, 0, 1024))
+            act(v(XN, 2048, 3584), xl(2048, 3584), ACT.Copy)
+            copy(v(XN, 1024, 2048), xl(1024, 2048))
+            dma(v("y", 1024, 2048), v(XN, 1024, 2048))
+            tt(SZ, v("b7", 0, 256), v("REM"), OP.min)
+            tt(v("T1"), v("VC"), SZ, OP.add)
+            dma(v("y", 2048, 3584), v(XN, 2048, 3584))
+            dma(v("ye", 0, 4096, 1, (0, 8, 1)), v("T1"))
+            dma(v("y", 3584, 4096), v(XN, 3584, 4096))
+
+    qidx = {}
+    hist = {}
+    known = {}
+    need = set()
+    for k, o in enumerate(ops):
+        q = o["q"]
+        o["k"] = k
+        if o["sem"] is None:
+            o["tok"] = (q, qidx.get(q, 0))
+            qidx[q] = qidx.get(q, 0) + 1
+        else:
+            o["tok"] = ("*" + o["sem"], 0)
+        deps = []
+        for wr, lst in ((0, o["r"]), (1, o["w"])):
+            for x in lst:
+                name = x[0]
+                psum = name[0] == "b" and len(name) == 2
+                m = pm(x[1])
+                keep = []
+                for h in hist.get(name, []):
+                    ho, hw, hx = h
+                    over = (pm(hx[1]) & m) and hx[2] < x[3] and x[2] < hx[3]
+                    same = ho["q"] == q and o["sem"] is None and ho["sem"] is None
+                    if psum and not same:
+                        deps.append(ho)
+                    elif psum and q == "P":
+                        pass
+                    elif over and (wr or hw):
+                        deps.append(ho)
+                    if wr and not psum and hx[2] >= x[2] and hx[3] <= x[3] and (pm(hx[1]) & ~m) == 0 and x[4] == 1:
+                        continue
+                    keep.append(h)
+                if psum and len(keep) > 200:
+                    keep = keep[-200:]
+                hist[name] = keep
+        kn = known.setdefault(q if q != "R" else ("R", k), {})
+        waits = []
+        best = {}
+        for ho in deps:
+            tq, ti = ho["tok"]
+            if tq not in best or best[tq]["tok"][1] < ti:
+                best[tq] = ho
+        for ho in sorted(best.values(), key=lambda z: -z["k"]):
+            tq, ti = ho["tok"]
+            if kn.get(tq, -1) >= ti:
+                continue
+            waits.append(ho)
+            need.add(ho["tok"])
+            for a, b in ho["kn"].items():
+                if kn.get(a, -1) < b:
+                    kn[a] = b
+            kn[tq] = max(kn.get(tq, -1), ti)
+        o["waits"] = waits
+        o["kn"] = dict(kn)
+        for wr, lst in ((0, o["r"]), (1, o["w"])):
+            for x in lst:
+                hist.setdefault(x[0], []).append((o, wr, x))
+    cnt = {}
+    eng_of = {"V": g.vector, "S": g.scalar, "P": g.tensor, "G": g, "Y": g.sync}
+    sem_of = {"V": "sV", "S": "sS", "P": "sP", "G": "sG"}
+    for o in ops:
+        q = o["q"]
+        if q == "R":
+            o["val"] = o["n"]
+            continue
+        e = eng_of[q]
+        for ho in o["waits"]:
+            e.wait_ge(T.sem[ho["sem"] or sem_of[ho["q"]]], ho["val"])
+        r = o["call"]()
+        if o["sem"] is not None:
+            o["val"] = o["n"]
+            if q != "G":
+                r.then_inc(T.sem[o["sem"]], o["n"])
+        elif o["tok"] in need:
+            cnt[q] = cnt.get(q, 0) + 1
+            o["val"] = cnt[q]
+            r.then_inc(T.sem[sem_of[q]], 1)
+    for q in ("V", "S", "P", "G"):
+        if cnt.get(q, 0):
+            g.wait_ge(T.sem[sem_of[q]], cnt[q])
+    for o in ops:
+        if o["sem"] is not None:
+            g.wait_ge(T.sem[o["sem"]], o["n"])

@@ -38,22 +38,22 @@ for _t in range(RO + 1):
     SCRATCH["X%d" % _t] = ("sbuf", [128, 4112], "bfloat16")
 for _t in range(RO):
     SCRATCH["LZ%d" % _t] = ("sbuf", [128, 512], "bfloat16")
-for _n in ("LP", "LN", "LB", "L1", "L2", "L3", "L4", "LV", "SELH"):
+for _n in ("LP", "LN", "LB", "L1", "L2", "L3", "L4", "SELH"):
     SCRATCH[_n] = ("sbuf", [128, 2048], "bfloat16")
-for _n in ("ID", "TRI", "TRI2", "SHF", "ONE", "CODE", "MISS", "NV", "MM", "DD", "GQ", "AF0", "AF1"):
+for _n in ("ID", "TRI", "TRI2", "SHF", "ONE", "CODE", "MISS", "NV", "MM", "GQ", "NID", "AF0", "AF1"):
     SCRATCH[_n] = ("sbuf", [128, 128], "float32")
 for _n in ("PKI", "PPI", "PSI"):
     SCRATCH[_n] = ("sbuf", [128, 256], "int32")
 for _n in ("TI", "THI", "TLO"):
     SCRATCH[_n] = ("sbuf", [128, 128], "int32")
-for _n in ("HIb", "LOb"):
+for _n in ("HIb", "LOb", "IDB", "NIDB", "ID2B", "ID64"):
     SCRATCH[_n] = ("sbuf", [128, 128], "bfloat16")
-for _n in ("VG", "VC", "REM", "QW", "ZERO", "KD", "TW", "TWE", "HF", "EG", "HK", "HINC", "A1", "KB", "VGK",
-           "OX", "OUT", "KI", "POS", "S2", "T1", "T2", "T3", "T4", "T5", "T6"):
+for _n in ("VG", "VC", "REM", "QW", "ZERO", "KD", "TW", "TWE", "HF", "EG", "HK", "HINC", "HEC", "KDE", "CK", "CV",
+           "OX", "OUT", "KI", "POS", "T1", "T2", "T3", "T4", "T5", "T6"):
     SCRATCH[_n] = ("sbuf", [128, 256], "float32")
 for _n in ("SZ", "HM", "HME", "RS", "J2", "EF"):
     SCRATCH[_n] = ("sbuf", [128, 264], "float32")
-for _n in ("B0", "B1", "H0", "H1", "HMb", "J0", "J1", "P0", "P1", "S20", "S21", "Z0", "Z1"):
+for _n in ("B0", "B1", "H0", "H1", "HMb", "J0", "J1", "P0", "P1", "Z0", "Z1", "S20", "S21"):
     SCRATCH[_n] = ("sbuf", [128, 256], "bfloat16")
 for _n in range(8):
     SCRATCH["b%d" % _n] = ("psum", [128, 512], "float32")
@@ -236,7 +236,7 @@ def rank_program(g, core, T, topo):
         tt(v("T3"), v("KD"), v("VC"), OP.add)
         tt(v("T2"), v("TW"), SZ1, OP.mult)
         tt(v("T4"), v("T2"), v("T3"), OP.add)
-        act(v("B0"), v("T4"), ACT.Copy)
+        copy(v("B0"), v("T4"))
         rows("INFO", 0, 1, "B0")
         tt(v("B1"), v("T4"), v("B0"), OP.subtract)
         rows("INFO", 1, 1, "B1")
@@ -247,6 +247,7 @@ def rank_program(g, core, T, topo):
         tt(v("EG"), v("VG"), SZ, OP.add)
         ts(v("HF"), v("KD"), -1.0, OP.mult, 1.0, OP.add)
         tt(v("TWE"), v("TW"), v("EG"), OP.mult)
+        tt(v("KDE"), v("KD"), v("EG"), OP.mult)
 
     tt(SZ, v("EI"), v("VC"), OP.subtract)
     tables()
@@ -265,16 +266,11 @@ def rank_program(g, core, T, topo):
         else:
             act(v(name), v("LP"), ACT.Copy, None, c)
     weight("LB", 8, [(0, 1), (1, 1)], True)
-    ts(v("LN"), v("LP"), -1.0, OP.mult)
-    weight("L1", 9, [(0, 1), (1, 1), (2, 8192)], False)
-    weight("L2", 10, [(3, 1), (4, 1)], False)
-    weight("L3", 11, [(0, 4096), (1, 4096), (2, 0.5), (3, 0.5)], False)
-    weight("L4", 13, [(4, 1), (5, 1)], True)
-    weight("LV", 14, [(0, 64), (1, 1)], True)
+    act(v("LN"), v("LP"), ACT.Copy, None, -1.0)
     ts(col(4), II, 14.0, OP.is_ge, 512.0, OP.mult)
     ts(v("REM"), v("VC"), col(4), OP.subtract, -1.0, OP.mult)
     ts(v("REM"), v("REM"), 3584.0, OP.add)
-    fill(v("SELH"), 1.0)
+    iota(v("SELH"), [[0, 2048]], 1, 0)
     iota(v("TRI"), [[16, 8], [0, 16]], 0, 0)
     iota(v("QW"), [[16, 256]], 0, 1)
     ts(v("QW"), v("QW"), G16, OP.subtract)
@@ -283,10 +279,13 @@ def rank_program(g, core, T, topo):
     ts(v("TRI2"), v("TRI"), 2.0, OP.mult)
     asel(v("SELH"), v("SELH"), [[128, 4], [-1, 4], [-4, 128]], OP.is_equal, 0.0, 0, 1)
     iota(v("GH"), [[0, 4128]], 0, 0)
-    iota(v("BIG", 0, 4096), [[1, 4], [0, 64], [4, 16]], 1, 0)
-    iota(v("VPAY"), [[0, 4], [1, 64], [0, 16]], 1, 0)
+    iota(v("BIG", 0, 4096), [[0, 16], [1, 16], [0, 16]], 0, -1)
+    iota(v("VPAY"), [[1, 16], [0, 16], [16, 16]], 0, 0)
     iota(v("GV"), [[0, 4096]], 0, 0)
-    dma(v("VPAY", 0, 4096, 1, (0, 128, 16)), v("BIG", 0, 4096, 1, (0, 128, 16)))
+    for name, k in (("IDB", 1.0), ("NIDB", -1.0), ("ID2B", 2.0), ("ID64", 65536.0), ("NID", -1.0)):
+        act(v(name), v("ID"), ACT.Copy, None, k)
+    ts(v("CK"), v("VC"), GB2, OP.subtract)
+    ts(v("CV"), v("VC"), -1.0, OP.mult, 12288.0, OP.add)
 
     IG = (0, 1024)
     TA = (2048, 3072)
@@ -321,12 +320,11 @@ def rank_program(g, core, T, topo):
             act(big(RB, h), big(TB, h), ACT.Relu, None, -1.0)
             bwd(v("b%d" % (2 + h), 0, 64), "LP", "BIG", BO + RB[h], 64, False, True)
             tt(w64("MM", h), v("b%d" % h, 0, 64), w64(AFn[s % 2], h), OP.min)
-            tt(w64("DD", h), v("b%d" % h, 0, 64), w64("MM", h), OP.subtract)
 
         def decide(h, s):
             ts(w64("GQ", h), v("b%d" % (2 + h), 0, 64), 0.0, OP.is_gt)
-            tt(w64("GQ", h), w64("GQ", h), w64("DD", h), OP.mult)
-            tt(w64("NV", h), w64("GQ", h), w64("MM", h), OP.add)
+            tt(w64("GQ", h), w64("GQ", h), v("b%d" % h, 0, 64), OP.mult)
+            tt(w64("NV", h), w64("GQ", h), w64("MM", h), OP.max)
             if s < 3:
                 ts(w64("AL", h), w64("NV", h), 1.0, OP.add)
                 ts(w64(AFn[(s + 1) % 2], h), w64("NV", h), 1.0, OP.add)
@@ -334,10 +332,12 @@ def rank_program(g, core, T, topo):
                 tt(w64("MISS", h), w64(AFn[0], h), w64(AFn[1], h), OP.is_le)
                 ts(w64("MISS", h), w64("MISS", h), 8192.0, OP.mult)
 
-        for h in range(2):
-            s0 = v("STI", 128 * t + 64 * h, 128 * t + 64 * h + 64)
-            ts(w64("AL", h), s0, 1.0, OP.add)
-            ts(w64("AF0", h), s0, 1.0, OP.add)
+        def starts(t):
+            s0 = v("STI", 128 * t, 128 * t + 128)
+            ts(v("AL"), s0, 1.0, OP.add)
+            ts(v("AF0"), s0, 1.0, OP.add)
+        if t == 0:
+            starts(0)
         info(0)
         info(1)
         for s in range(4):
@@ -354,12 +354,6 @@ def rank_program(g, core, T, topo):
                 first_kid(1)
                 first_sum(1)
             second_kid(1, s)
-            if s == 0:
-                tables2()
-            if s == 1:
-                copy(v("EF", 256, 257), v("b6", 0, 1))
-                copy(v("EL", 0, 257), v("EF", 0, 257))
-                iota(v("BIG", 0, 4096), [[0, 4096]], 0, 0)
             decide(0, s)
             if s < 3:
                 info(0)
@@ -379,10 +373,30 @@ def rank_program(g, core, T, topo):
         for n in range(NLO):
             ts(bg(8192 + 128 * n, 8192 + 128 * n + 128), v("LOb"), float(n), OP.is_equal)
         fill(bg(16384, 16512), -1.0)
+        mm(v("b0", 0, 256), v("ID"), v("CK"), True, False)
+        mm(v("b1", 0, 256), v("ID"), v("CV"), True, False)
+        mm(v("b2", 0, 256), v("ID"), v("VG"), True, False)
+        mm(v("b3", 0, 256), v("ID"), SZ, True, False)
+        tables2()
+        if t < RO - 1:
+            starts(t + 1)
+
+        def payload(a, b):
+            if t == 0:
+                tt(v("VPAY", a, b), v("VPAY", a, b), v("BIG", a, b), OP.add)
+        if t == 0:
+            weight("L1", 9, [(0, 1), (1, 1), (2, 8192)], False)
+            weight("L2", 10, [(3, 1), (4, 1)], False)
+            weight("L3", 11, [(0, 4096), (1, 4096), (2, 0.5), (3, 0.5)], False)
+            weight("L4", 13, [(4, 1), (5, 1)], False)
+            ts(v("BIG", 0, 4096), v("BIG", 0, 4096), G16, OP.add, 0.0, OP.is_ge)
+        payload(0, 2048)
         for gg in range(8):
             for i in range(16):
                 c = 16 * gg + i
                 mm(v("b4", gg // 2, 260, 4, (64 * (gg % 2), 64 * (gg % 2) + 64, 1)), bg(c, 8192, 128), bg(8192 + c, 16512, 128), i == 0, i == 15)
+        copy(v("EF", 256, 257), v("b6", 0, 1))
+        copy(v("EL", 0, 257), v("EF", 0, 257))
         copy(v("T1"), v("b4", 4, 260))
         copy(v("HB", 0, 4 * NLO), v("b4", 0, 4 * NLO))
         tt(v("HB", 4 * NLO, 256), v("b4", 4 * NLO, 256), v("T1", 4 * NLO, 256), OP.subtract)
@@ -393,7 +407,7 @@ def rank_program(g, core, T, topo):
         tt(HM, v("b5", 0, 256), v("HF"), OP.min)
         red(v("RC", 0, 1), HM, OP.add)
         mm(v("b6", 2, 3), v("TRI"), v("RC", 0, 1), True, True)
-        copy(v("HMb"), HM)
+        act(v("HMb"), HM, ACT.Copy)
         rows("GH", 2, 15, "HMb")
         scan(v("HINC"), v("ZERO"), HM, v("b6", 2, 3), OP.add, OP.add)
         copy(v("H0"), v("HINC"))
@@ -401,10 +415,14 @@ def rank_program(g, core, T, topo):
         tt(v("H1"), v("HINC"), v("H0"), OP.subtract)
         rows("GH", 1, 16, "H1")
         edge("HM")
-        tt(v("HK"), v("HM", 1, 257), v("KD"), OP.mult)
-        tt(v("HK"), v("HK"), v("EG"), OP.mult)
-        ts(v("VGK"), HM, 65536.0, OP.mult)
-        tt(v("VGK"), v("VGK"), v("VG"), OP.add)
+        tt(v("HK"), v("HM", 1, 257), v("KDE"), OP.mult)
+        mm(v("b2", 0, 256), v("ID64"), v("HMb"), False, True)
+        mm(v("b1", 0, 256), v("ID2B"), v("H0"), False, False)
+        mm(v("b1", 0, 256), v("ID2B"), v("H1"), False, True)
+        tt(v("T2"), HM, v("b1", 0, 256), OP.mult)
+        payload(2048, 2816)
+        mm(v("b0", 0, 256), v("NIDB"), v("H0"), False, False)
+        mm(v("b0", 0, 256), v("NIDB"), v("H1"), False, False)
         for k in (0, 2, 1, 3):
             w = 65 if k == 3 else 64
             o, i = v("G1", 1024 * k, 1024 * k + 16 * w), ind(v("GH", 16, 4112), v("EL", 64 * k, 64 * k + w))
@@ -413,11 +431,12 @@ def rank_program(g, core, T, topo):
             else:
                 act(o, i, ACT.Copy)
             bwd(v("b7", 64 * k, 64 * k + w), "L1", "G1", 1024 * k, w)
-        ts(v("T2"), v("HINC"), 2.0, OP.mult, 12288.0, OP.add)
-        tt(v("T2"), v("T2"), v("VC"), OP.subtract)
-        tt(v("T2"), v("T2"), HM, OP.mult)
-        tt(v("KB"), v("VC"), v("HINC"), OP.subtract)
-        tt(v("KB"), v("KB"), v("T2"), OP.add)
+        mm(v("b0", 0, 256), v("ID"), v("T2"), False, True)
+        mm(v("b3", 0, 256), v("IDB"), v("H0"), False, False)
+        mm(v("b3", 0, 256), v("IDB"), v("H1"), False, False)
+        mm(v("b3", 0, 256), v("NIDB"), v("HMb"), False, False)
+        payload(2816, 4096)
+        iota(v("BIG", 0, 4096), [[0, 4096]], 0, 0)
         ts(v("HME", 0, 257), v("b7", 0, 257), 8192.0, OP.is_ge)
         tt(v("T4"), v("TWE"), v("HME", 1, 257), OP.mult)
         tt(v("T4"), v("T4"), v("HK"), OP.max)
@@ -432,12 +451,12 @@ def rank_program(g, core, T, topo):
             scan(out, src, src, v("b6", ini, ini + 1), OP.max, OP.max)
 
         def f1():
-            ts(v("T2"), v("HME", 0, 256), -8192.0, OP.mult)
+            ts(v("HEC"), v("HME", 0, 256), -8192.0, OP.mult)
 
         def f2():
-            tt(v("T2"), v("T2"), v("b7", 0, 256), OP.add)
+            tt(v("HEC"), v("HEC"), v("b7", 0, 256), OP.add)
         maxscan(v("RS", 1, 257), v("T4"), 1, 4, (f1, f2))
-        tt(v("KI"), v("RS", 1, 257), v("VGK"), OP.is_gt)
+        tt(v("KI"), v("RS", 1, 257), v("b2", 0, 256), OP.is_gt)
         red(v("RC", 2, 3), v("KI"), OP.add)
         mm(v("b6", 6, 7), v("ID"), GB2, True, False)
         mm(v("b6", 6, 7), v("TRI2"), v("RC", 2, 3), False, True)
@@ -454,43 +473,42 @@ def rank_program(g, core, T, topo):
             rows("GH", 4, 16, "J1")
 
         def f4():
-            ts(v("KB"), v("KB"), GB2, OP.subtract)
+            ts(v("OUT"), v("KI"), -1.0, OP.mult, 1.0, OP.add)
         maxscan(v("T6"), v("T5"), 3, 8, (f3, f4))
-        tt(v("POS"), v("KB"), v("T6"), OP.add)
+        tt(v("POS"), v("b0", 0, 256), v("T6"), OP.add)
         copy(v("OFF"), v("POS"))
         act(v("P0"), v("POS"), ACT.Copy)
         rows("GV", 0, 0, "P0")
-        tt(v("S2"), v("J2", 1, 257), v("T6"), OP.subtract)
-        act(v("S20"), v("S2"), ACT.Copy)
+        mm(v("b1", 0, 256), v("IDB"), v("J0"), True, False)
+        mm(v("b1", 0, 256), v("IDB"), v("J1"), False, False)
+        mm(v("b1", 0, 256), v("NID"), v("T6"), False, True)
+        act(v("S20"), v("b1", 0, 256), ACT.Copy)
         rows("GV", 2, 0, "S20")
-        copy(ind(v("BIG", 0, 20480), v("OFF")), v("VPAY"))
-        for k in range(4):
-            act(v("G1", 1024 * k, 1024 * k + 1024), ind(v("GH", 16, 4112), v("EL", 64 * k, 64 * k + 64)), ACT.Copy)
-            bwd(v("b5", 256 + 64 * k, 256 + 64 * k + 64), "L2", "G1", 1024 * k, 64)
         tt(v("P1"), v("POS"), v("P0"), OP.subtract)
         rows("GV", 1, 0, "P1")
-        tt(v("S21"), v("S2"), v("S20"), OP.subtract)
+        copy(ind(v("BIG", 0, 20480), v("OFF", 0, 192)), v("VPAY", 0, 3072))
+        mm(v("b3", 0, 256), v("NID"), v("HEC"), False, True)
+        mm(v("b5", 0, 256), v("NID"), v("J2", 0, 256), True, False)
+        for k in range(4):
+            act(v("G1", 1024 * k, 1024 * k + 1024), ind(v("GH", 16, 4112), v("EL", 64 * k, 64 * k + 64)), ACT.Copy)
+            bwd(v("b5", 64 * k, 64 * k + 64), "L2", "G1", 1024 * k, 64, False, k == 3)
+        tt(v("S21"), v("b1", 0, 256), v("S20"), OP.subtract)
         rows("GV", 3, 0, "S21")
-        ts(bg(0, 2560), v("BIG", 0, 2560), 0.0, OP.is_equal)
-        act(bg(2560, 4096), v("BIG", 2560, 4096), ACT.Relu, 1.0, -1.0)
-        tt(v("A1"), SZ, v("HINC"), OP.add)
-        tt(v("A1"), v("A1"), HM, OP.subtract)
-        tt(v("A1"), v("A1"), v("T2"), OP.subtract)
-        tt(v("OUT"), v("RS", 1, 257), v("VG"), OP.is_le)
-        tt(v("T5"), v("b5", 256, 512), v("J2", 0, 256), OP.subtract)
-        tt(v("T5"), v("T5"), v("OUT"), OP.mult)
-        tt(v("T5"), v("T5"), v("A1"), OP.add)
+        tt(v("T5"), v("OUT"), v("b5", 0, 256), OP.mult)
+        tt(v("T5"), v("T5"), v("b3", 0, 256), OP.add)
         act(v("Z0"), v("T5"), ACT.Copy)
         rows("GV", 4, 0, "Z0")
+        tt(v("Z1"), v("T5"), v("Z0"), OP.subtract)
+        rows("GV", 5, 0, "Z1")
+        copy(ind(v("BIG", 0, 20480), v("OFF", 192, 256)), v("VPAY", 3072, 4096))
         for k in range(4):
             a = 1024 * k
-            scan(v("VLS", a, a + 1024), bg(a, a + 1024), v("BIG", a, a + 1024), 0.0 if k == 0 else v("VLS", a - 1, a), OP.mult, OP.add)
-            bwd(v("b%d" % k, 0, 64), "LV", "VLS", a, 64)
-            if k == 0:
-                tt(v("Z1"), v("T5"), v("Z0"), OP.subtract)
-                rows("GV", 5, 0, "Z1")
-        for k in range(4):
-            ts(v("VLL", 64 * k, 64 * k + 64), v("b%d" % k, 0, 64), -65.0, OP.add)
+            scan(v("VLS", a, a + 1024), v("BIG", a, a + 1024), v("BIG", a, a + 1024), 0.0 if k == 0 else v("VLS", a - 1, a), OP.max, OP.max)
+            bwd(v("b%d" % k, 0, 64), "LP", "VLS", a, 64)
+            if k == 2:
+                ts(v("VLL", 0, 64), v("b0", 0, 64), -1.0, OP.add)
+        for k in range(1, 3):
+            ts(v("VLL", 64 * k, 64 * k + 64), v("b%d" % k, 0, 64), -1.0, OP.add)
 
         def gat(k, out, win):
             i = ind(win, v("VLL", 64 * k, 64 * k + 64))
@@ -500,11 +518,14 @@ def rank_program(g, core, T, topo):
                 copy(out, i)
         for k in (0, 2, 1, 3):
             a = 1024 * k
+            if k == 3:
+                ts(v("VLL", 192, 256), v("b3", 0, 64), -1.0, OP.add)
             gat(k, bg(12288 + a, 12288 + a + 1024), v("GV"))
             bwd(v("b4", 64 * k, 64 * k + 64), "L3", "BIG", BO + 12288 + a, 64)
         for k in (0, 2, 1, 3):
             gat(k, bg(1024 * k, 1024 * k + 1024), v(X))
         act(bg(4096, 6144), bg(0, 2048), ACT.Relu, -1.0)
+        act(bg(6144, 8192), bg(2048, 4096), ACT.Relu, -1.0)
         copy(v("PKI"), v("b4", 0, 256))
         ts(v("PPI"), v("PKI"), 12, OP.arith_shift_right)
         ts(v("PSI"), v("PKI"), 4095, OP.bitwise_and)
@@ -515,10 +536,6 @@ def rank_program(g, core, T, topo):
         tt(v("T4"), v("T3"), v("PSI"), OP.mult)
         tt(v("T4"), v("QW"), v("T4"), OP.subtract)
         copy(v("QL"), v("T4"))
-        ts(v("T3"), v("T3"), 4096.0, OP.mult)
-        tt(v("T5"), v("T3"), v("T4"), OP.add)
-        copy(v("XL"), v("T5"))
-        act(bg(6144, 8192), bg(2048, 4096), ACT.Relu, -1.0)
         dst = T.cores[(rank + 1) % len(T.cores)]
         src = T.cores[(rank - 1) % len(T.cores)]
 
@@ -547,10 +564,14 @@ def rank_program(g, core, T, topo):
             sizes(v("SZB", 512 * k, 512 * k + 512), 512 * k, 512 * k + 512, k < 3)
             szc(2 * k)
             szc(2 * k + 1)
+            if k == 0:
+                ts(v("T3"), v("T3"), 4096.0, OP.mult)
+                tt(v("T5"), v("T3"), v("T4"), OP.add)
+                copy(v("XL"), v("T5"))
         szc(14)
         szc(15)
         ts(bg(8192, 12288), bg(0, 4096), 2.0, OP.subtract, 0.0, OP.max)
-        copy(v("XS"), xl(3584, 4096))
+        act(v("XS"), xl(3584, 4096), ACT.Copy)
         send("XS", v(XN, 3584, 4096), "rx%d" % t, "lx%d" % t)
         if t < RO - 1:
             act(v(XN, 1024, 3584), xl(1024, 3584), ACT.Copy)

import numpy as np
from concourse.bass import DstId, RemoteDMATransfer
from concourse.mybir import dt, AluOpType, AxisListType, ActivationFunctionType
import comms_topo

RO = 3
NLO = 20

SCRATCH = {
    "BIG": ("sbuf", [128, 20736], "bfloat16"),
    "VPAY": ("sbuf", [128, 4096], "bfloat16"),
    "WP": ("sbuf", [128, 2048], "bfloat16"),
    "INFO": ("sbuf", [128, 4112], "bfloat16"),
    "GH": ("sbuf", [128, 4128], "bfloat16"),
    "GV": ("sbuf", [128, 4096], "bfloat16"),
    "G1": ("sbuf", [128, 4112], "bfloat16"),
    "VLS": ("sbuf", [128, 4096], "bfloat16"),
    "SZB": ("sbuf", [128, 3584], "bfloat16"),
    "XS": ("sbuf", [128, 512], "bfloat16"),
    "SZS": ("sbuf", [128, 512], "bfloat16"),
    "HB": ("sbuf", [128, 256], "bfloat16"),
    "STI": ("sbuf", [128, 384], "int32"),
    "EI": ("sbuf", [128, 256], "int32"),
    "AL": ("sbuf", [128, 128], "uint16"),
    "BL": ("sbuf", [128, 128], "uint16"),
    "EL": ("sbuf", [128, 264], "uint16"),
    "OFF": ("sbuf", [128, 256], "uint16"),
    "VLL": ("sbuf", [128, 256], "uint16"),
    "QL": ("sbuf", [128, 256], "uint16"),
    "XL": ("sbuf", [128, 256], "uint16"),
    "PI": ("sbuf", [128, 4], "int32"),
    "COL": ("sbuf", [128, 32], "float32"),
    "ROW": ("sbuf", [128, 160], "float32"),
    "ROW2": ("sbuf", [128, 160], "float32"),
    "RC": ("sbuf", [128, 8], "float32"),
}
for _t in range(RO + 1):
    SCRATCH["X%d" % _t] = ("sbuf", [128, 4112], "bfloat16")
for _t in range(RO):
    SCRATCH["LZ%d" % _t] = ("sbuf", [128, 512], "bfloat16")
for _n in ("LP", "LN", "LB", "L1", "L2", "L3", "L4", "SELH"):
    SCRATCH[_n] = ("sbuf", [128, 2048], "bfloat16")
for _n in ("ID", "TRI", "TRI2", "SHF", "ONE", "CODE", "MISS", "NV", "MM", "GQ", "NID", "AF0", "AF1"):
    SCRATCH[_n] = ("sbuf", [128, 128], "float32")
for _n in ("PKI", "PPI", "PSI"):
    SCRATCH[_n] = ("sbuf", [128, 256], "int32")
for _n in ("TI", "THI", "TLO"):
    SCRATCH[_n] = ("sbuf", [128, 128], "int32")
for _n in ("HIb", "LOb", "IDB", "NIDB", "ID2B", "ID64"):
    SCRATCH[_n] = ("sbuf", [128, 128], "bfloat16")
for _n in ("VG", "VC", "REM", "QW", "ZERO", "KD", "TW", "TWE", "HF", "EG", "HK", "HINC", "HEC", "KDE", "CK", "CV",
           "OX", "OUT", "KI", "POS", "T1", "T2", "T3", "T4", "T5", "T6"):
    SCRATCH[_n] = ("sbuf", [128, 256], "float32")
for _n in ("SZ", "HM", "HME", "RS", "J2", "EF"):
    SCRATCH[_n] = ("sbuf", [128, 264], "float32")
for _n in ("B0", "B1", "H0", "H1", "HMb", "J0", "J1", "P0", "P1", "Z0", "Z1", "S20", "S21"):
    SCRATCH[_n] = ("sbuf", [128, 256], "bfloat16")
for _n in range(8):
    SCRATCH["b%d" % _n] = ("psum", [128, 512], "float32")

SEMAPHORES = (["sV", "sS", "sP", "sG"] + ["d%d" % _k for _k in range(72)]
              + ["%s%d" % (_a, _k) for _a in ("rx", "rz", "lx", "lz") for _k in range(RO)])

ALL = (0, 128, 1)
ONEROW = (0, 1, 1)
ACT = ActivationFunctionType
OP = AluOpType


def v(name, c0=0, c1=None, cs=1, p=ALL):
    if c1 is None:
        c1 = 4096 if name in ("y", "ye", "x", "ends") else SCRATCH[name][1][1]
    return (name, p, c0, c1, cs)


BO = 4096


def bg(c0, c1, cs=1):
    return v("BIG", BO + c0, BO + c1, cs)


def ind(win, off):
    return ("@", win, off)


def pmask(p):
    m = 0
    for k in range(p[0], p[1], p[2]):
        m |= 1 << k
    return m


def rank_program(g, core, T, topo):
    rank = T.rank_of(core)
    if rank is None:
        return
    ops = []
    masks = {}

    def pm(p):
        if p not in masks:
            masks[p] = pmask(p)
        return masks[p]

    def flat(x, out):
        if isinstance(x, tuple):
            if x[0] == "@":
                out.append(x[1])
                out.append(x[2])
            elif len(x) == 5:
                out.append(x)
        return out

    def add(q, reads, writes, call, sem=None, n=1):
        rd = []
        for x in reads:
            flat(x, rd)
        wr = []
        for x in writes:
            if x[0] == "@":
                wr.append(x[1])
                rd.append(x[2])
            else:
                wr.append(x)
        ops.append({"q": q, "r": rd, "w": wr, "call": call, "sem": sem, "n": n})

    def ap(x):
        if not isinstance(x, tuple):
            return x
        if x[0] == "@":
            return ap(x[1]).indirect(ap(x[2]))
        name, p, c0, c1, cs = x
        return T[name][p[0]:p[1]:p[2], c0:c1:cs] if (p[2] != 1 or cs != 1) else T[name][p[0]:p[1], c0:c1]

    def copy(out, i):
        add("V", [i], [out], lambda: g.vector.tensor_copy(ap(out), ap(i)))

    def tt(out, a, b, op):
        add("V", [a, b], [out], lambda: g.vector.tensor_tensor(ap(out), ap(a), ap(b), op))

    def ts(out, a, s1, op0, s2=None, op1=None):
        if op1 is None:
            add("V", [a, s1], [out], lambda: g.vector.tensor_scalar(ap(out), ap(a), ap(s1), None, op0))
        else:
            add("V", [a, s1, s2], [out], lambda: g.vector.tensor_scalar(ap(out), ap(a), ap(s1), ap(s2), op0, op1))

    def red(out, i, op):
        add("V", [i], [out], lambda: g.vector.tensor_reduce(ap(out), ap(i), AxisListType.X, op))

    def scan(out, d0, d1, init, op0, op1):
        add("V", [d0, d1, init], [out], lambda: g.vector.tensor_tensor_scan(ap(out), ap(d0), ap(d1), ap(init), op0, op1))

    def fill(out, c):
        add("V", [], [out], lambda: g.vector.memset(ap(out), c))

    def act(out, i, func, bias=None, scale=None):
        def call():
            kw = {}
            if bias is not None:
                kw["bias"] = bias
            if scale is not None:
                kw["scale"] = ap(scale)
            return g.scalar.activation(ap(out), ap(i), func, **kw)
        add("S", [i, scale], [out], call)

    def mm(out, l, r, start, stop):
        add("P", [l, r], [out], lambda: g.tensor.matmul(ap(out), ap(l), ap(r), start, stop))

    def tr(out, i, idn):
        add("P", [i, idn], [out], lambda: g.tensor.transpose(ap(out), ap(i), ap(idn)))

    def iota(out, pattern, base, cm, small=True):
        if small:
            add("G", [], [out], lambda: g.iota(ap(out), pattern, base, cm, allow_small_or_imprecise_dtypes=True))
        else:
            add("G", [], [out], lambda: g.iota(ap(out), pattern, base, cm))

    def asel(out, i, pattern, cop, fillv, base, cm):
        add("G", [i], [out], lambda: g.affine_select(ap(out), ap(i), pattern, cop, fillv, base, cm))

    nd = [0]

    def dma(out, i):
        sem = "d%d" % nd[0]
        nd[0] += 1
        add("Y", [i], [out], lambda: g.sync.dma_start(ap(out), ap(i)), sem, 16)

    def rows(name, r, c0, src):
        dma(v(name, c0, c0 + 4096, 1, (r, 128, 16)), v(src))

    def bwd(out, lname, src, c0, k, first=True, last=True):
        for i in range(16):
            mm(out, v(lname, 128 * i, 128 * i + 128), v(src, c0 + i, c0 + 16 * k, 16), first and i == 0, last and i == 15)

    dma(v("EI"), v("ends", 0, 4096, 1, (0, 8, 1)))
    dma(v("STI"), v("start", 0, 384))
    dma(v("X0", 0, 4096), v("x"))
    dma(v("WP"), v("w", 0, 2048))
    PIc = v("PI", 0, 1)

    def col(k):
        return v("COL", k, k + 1)
    iota(PIc, [[0, 1]], 0, 1, False)
    iota(v("VG"), [[1, 256]], 0, 256)
    iota(bg(0, 2048), [[-1, 16], [1, 128]], 0, 0)
    fill(v("ONE"), 1.0)
    fill(v("INFO"), 0.0)
    asel(v("SHF"), v("ONE"), [[-1, 128]], OP.is_equal, 0.0, -1, 1)
    asel(v("ID"), v("ONE"), [[-1, 128]], OP.is_equal, 0.0, 0, 1)
    ts(v("PI", 1, 2), PIc, 4, OP.arith_shift_right)
    ts(v("PI", 2, 3), PIc, 15, OP.bitwise_and)
    G16, GB, II, GB2 = col(0), col(1), col(2), col(3)
    ts(GB, v("PI", 1, 2), 4096.0, OP.mult)
    ts(v("VC"), v("VG"), GB, OP.subtract)
    ts(G16, v("PI", 1, 2), 16.0, OP.mult)
    ts(GB2, v("PI", 1, 2), 8192.0, OP.mult)
    copy(II, v("PI", 2, 3))
    for t in range(RO + 1):
        fill(v("X%d" % t, 4096, 4112), 0.0)
    fill(v("ZERO"), 0.0)
    fill(v("ROW"), 0.0)
    fill(v("ROW2"), 0.0)
    SZ = v("SZ", 0, 256)
    SZ1 = v("SZ", 1, 257)

    def edge(name):
        mm(v("b6", 0, 1), v("SHF"), v(name, 0, 1), True, True)
        copy(v(name, 256, 257), v("b6", 0, 1))

    def tables():
        ts(v("T1"), SZ, -1.0, OP.add)
        ts(v("KD"), v("T1"), 1.0, OP.min)
        edge("SZ")
        tt(v("TW"), SZ1, v("T1"), OP.is_lt)
        tt(v("T3"), v("KD"), v("VC"), OP.add)
        tt(v("T2"), v("TW"), SZ1, OP.mult)
        tt(v("T4"), v("T2"), v("T3"), OP.add)
        copy(v("B0"), v("T4"))
        rows("INFO", 0, 1, "B0")
        tt(v("B1"), v("T4"), v("B0"), OP.subtract)
        rows("INFO", 1, 1, "B1")

    def tables2():
        tt(v("EF", 0, 256), v("VC"), v("T1"), OP.add)
        mm(v("b6", 0, 1), v("SHF"), v("EF", 0, 1), True, True)
        tt(v("EG"), v("VG"), SZ, OP.add)
        ts(v("HF"), v("KD"), -1.0, OP.mult, 1.0, OP.add)
        tt(v("TWE"), v("TW"), v("EG"), OP.mult)
        tt(v("KDE"), v("KD"), v("EG"), OP.mult)

    tt(SZ, v("EI"), v("VC"), OP.subtract)
    tables()
    ts(v("LP"), bg(0, 2048), G16, OP.is_equal)

    def weight(name, k, terms, onv):
        c = col(k)
        for n, (row, wgt) in enumerate(terms):
            if n == 0:
                ts(c, II, float(row), OP.is_equal, float(wgt), OP.mult)
            else:
                ts(col(31), II, float(row), OP.is_equal, float(wgt), OP.mult)
                tt(c, c, col(31), OP.add)
        if onv:
            ts(v(name), v("LP"), c, OP.mult)
        else:
            act(v(name), v("LP"), ACT.Copy, None, c)
    weight("LB", 8, [(0, 1), (1, 1)], True)
    act(v("LN"), v("LP"), ACT.Copy, None, -1.0)
    ts(col(4), II, 14.0, OP.is_ge, 512.0, OP.mult)
    ts(v("REM"), v("VC"), col(4), OP.subtract, -1.0, OP.mult)
    ts(v("REM"), v("REM"), 3584.0, OP.add)
    iota(v("SELH"), [[0, 2048]], 1, 0)
    iota(v("TRI"), [[16, 8], [0, 16]], 0, 0)
    iota(v("QW"), [[16, 256]], 0, 1)
    ts(v("QW"), v("QW"), G16, OP.subtract)
    ts(v("TRI"), v("TRI"), G16, OP.is_equal)
    asel(v("TRI"), v("TRI"), [[1, 128]], OP.is_gt, 0.0, 0, -1)
    ts(v("TRI2"), v("TRI"), 2.0, OP.mult)
    asel(v("SELH"), v("SELH"), [[128, 4], [-1, 4], [-4, 128]], OP.is_equal, 0.0, 0, 1)
    iota(v("GH"), [[0, 4128]], 0, 0)
    iota(v("BIG", 0, 4096), [[0, 16], [1, 16], [0, 16]], 0, -1)
    iota(v("VPAY"), [[1, 16], [0, 16], [16, 16]], 0, 0)
    iota(v("GV"), [[0, 4096]], 0, 0)
    for name, k in (("IDB", 1.0), ("NIDB", -1.0), ("ID2B", 2.0), ("ID64", 65536.0), ("NID", -1.0)):
        act(v(name), v("ID"), ACT.Copy, None, k)
    ts(v("CK"), v("VC"), GB2, OP.subtract)
    ts(v("CV"), v("VC"), -1.0, OP.mult, 12288.0, OP.add)

    IG = (0, 1024)
    TA = (2048, 3072)
    RA = (9216, 4096)
    TB = (5120, 6144)
    RB = (7168, 8192)

    for t in range(RO):
        X, XN = "X%d" % t, "X%d" % (t + 1)
        AFn = ["AF0", "AF1"]

        def w64(name, h):
            return v(name, 64 * h, 64 * h + 64)

        def big(base, h):
            return bg(base[h], base[h] + 1024)

        def info(h):
            act(big(IG, h), ind(v("INFO", 0, 4112), w64("AL", h)), ACT.Copy)
            bwd(v("b%d" % h, 0, 64), "LB", "BIG", BO + IG[h], 64)

        def first_kid(h):
            tt(big(TA, h), ind(v(X), w64("AL", h)), v("WP", 1024 * h, 1024 * h + 1024), OP.subtract)
            act(big(RA, h), big(TA, h), ACT.Relu, None, -1.0)

        def first_sum(h):
            bwd(v("b%d" % (2 + h), 0, 64), "LN", "BIG", BO + RA[h], 64, True, False)

        def second_kid(h, s):
            copy(w64("BL", h), v("b%d" % h, 0, 64))
            tt(big(TB, h), ind(v(X), w64("BL", h)), v("WP", 1024 * h, 1024 * h + 1024), OP.subtract)
            act(big(RB, h), big(TB, h), ACT.Relu, None, -1.0)
            bwd(v("b%d" % (2 + h), 0, 64), "LP", "BIG", BO + RB[h], 64, False, True)
            tt(w64("MM", h), v("b%d" % h, 0, 64), w64(AFn[s % 2], h), OP.min)

        def decide(h, s):
            ts(w64("GQ", h), v("b%d" % (2 + h), 0, 64), 0.0, OP.is_gt)
            tt(w64("GQ", h), w64("GQ", h), v("b%d" % h, 0, 64), OP.mult)
            tt(w64("NV", h), w64("GQ", h), w64("MM", h), OP.max)
            if s < 3:
                ts(w64("AL", h), w64("NV", h), 1.0, OP.add)
                ts(w64(AFn[(s + 1) % 2], h), w64("NV", h), 1.0, OP.add)
            if s == 1:
                tt(w64("MISS", h), w64(AFn[0], h), w64(AFn[1], h), OP.is_le)
                ts(w64("MISS", h), w64("MISS", h), 8192.0, OP.mult)

        def starts(t):
            s0 = v("STI", 128 * t, 128 * t + 128)
            ts(v("AL"), s0, 1.0, OP.add)
            ts(v("AF0"), s0, 1.0, OP.add)
        if t == 0:
            starts(0)
        info(0)
        info(1)
        for s in range(4):
            first_kid(0)
            first_sum(0)
            if s > 0:
                decide(1, s - 1)
                info(1)
            else:
                first_kid(1)
                first_sum(1)
            second_kid(0, s)
            if s > 0:
                first_kid(1)
                first_sum(1)
            second_kid(1, s)
            decide(0, s)
            if s < 3:
                info(0)
        decide(1, 3)
        tt(v("CODE"), v("NV"), v("MISS"), OP.add)
        tr(v("b7", 0, 128), v("CODE"), v("ID"))
        copy(v("TI"), v("b7", 0, 128))
        ts(v("TLO"), v("TI"), 63, OP.bitwise_and)
        copy(v("LOb"), v("TLO"))
        ts(v("THI"), v("TI"), 6, OP.arith_shift_right)
        copy(v("HIb"), v("THI"))
        for k in range(64):
            ts(bg(128 * k, 128 * k + 128), v("HIb"), float(k), OP.is_equal)
            if NLO + k < 64:
                n = NLO + k
                act(bg(8192 + 128 * n, 8192 + 128 * n + 128), v("LOb"), ACT.Sign, 0.5 - n)
        for n in range(NLO):
            ts(bg(8192 + 128 * n, 8192 + 128 * n + 128), v("LOb"), float(n), OP.is_equal)
        fill(bg(16384, 16512), -1.0)
        mm(v("b0", 0, 256), v("ID"), v("CK"), True, False)
        mm(v("b1", 0, 256), v("ID"), v("CV"), True, False)
        mm(v("b2", 0, 256), v("ID"), v("VG"), True, False)
        mm(v("b3", 0, 256), v("ID"), SZ, True, False)
        tables2()
        if t < RO - 1:
            starts(t + 1)

        def payload(a, b):
            if t == 0:
                tt(v("VPAY", a, b), v("VPAY", a, b), v("BIG", a, b), OP.add)
        if t == 0:
            weight("L1", 9, [(0, 1), (1, 1), (2, 8192)], False)
            weight("L2", 10, [(3, 1), (4, 1)], False)
            weight("L3", 11, [(0, 4096), (1, 4096), (2, 0.5), (3, 0.5)], False)
            weight("L4", 13, [(4, 1), (5, 1)], False)
            ts(v("BIG", 0, 4096), v("BIG", 0, 4096), G16, OP.add, 0.0, OP.is_ge)
        payload(0, 2048)
        for gg in range(8):
            for i in range(16):
                c = 16 * gg + i
                mm(v("b4", gg // 2, 260, 4, (64 * (gg % 2), 64 * (gg % 2) + 64, 1)), bg(c, 8192, 128), bg(8192 + c, 16512, 128), i == 0, i == 15)
        copy(v("EF", 256, 257), v("b6", 0, 1))
        copy(v("EL", 0, 257), v("EF", 0, 257))
        copy(v("T1"), v("b4", 4, 260))
        copy(v("HB", 0, 4 * NLO), v("b4", 0, 4 * NLO))
        tt(v("HB", 4 * NLO, 256), v("b4", 4 * NLO, 256), v("T1", 4 * NLO, 256), OP.subtract)
        for cc in range(4):
            for gh in range(4):
                mm(v("b5", 64 * cc, 64 * cc + 64), v("SELH", 128 * (4 * gh + cc), 128 * (4 * gh + cc) + 128), v("HB", gh, 256, 4), gh == 0, gh == 3)
        HM = v("HM", 0, 256)
        tt(HM, v("b5", 0, 256), v("HF"), OP.min)
        red(v("RC", 0, 1), HM, OP.add)
        mm(v("b6", 2, 3), v("TRI"), v("RC", 0, 1), True, True)
        act(v("HMb"), HM, ACT.Copy)
        rows("GH", 2, 15, "HMb")
        scan(v("HINC"), v("ZERO"), HM, v("b6", 2, 3), OP.add, OP.add)
        copy(v("H0"), v("HINC"))
        rows("GH", 0, 16, "H0")
        tt(v("H1"), v("HINC"), v("H0"), OP.subtract)
        rows("GH", 1, 16, "H1")
        edge("HM")
        tt(v("HK"), v("HM", 1, 257), v("KDE"), OP.mult)
        mm(v("b2", 0, 256), v("ID64"), v("HMb"), False, True)
        mm(v("b1", 0, 256), v("ID2B"), v("H0"), False, False)
        mm(v("b1", 0, 256), v("ID2B"), v("H1"), False, True)
        tt(v("T2"), HM, v("b1", 0, 256), OP.mult)
        payload(2048, 2816)
        mm(v("b0", 0, 256), v("NIDB"), v("H0"), False, False)
        mm(v("b0", 0, 256), v("NIDB"), v("H1"), False, False)
        for k in (0, 2, 1, 3):
            w = 65 if k == 3 else 64
            o, i = v("G1", 1024 * k, 1024 * k + 16 * w), ind(v("GH", 16, 4112), v("EL", 64 * k, 64 * k + w))
            if k < 2:
                copy(o, i)
            else:
                act(o, i, ACT.Copy)
            bwd(v("b7", 64 * k, 64 * k + w), "L1", "G1", 1024 * k, w)
        mm(v("b0", 0, 256), v("ID"), v("T2"), False, True)
        mm(v("b3", 0, 256), v("IDB"), v("H0"), False, False)
        mm(v("b3", 0, 256), v("IDB"), v("H1"), False, False)
        mm(v("b3", 0, 256), v("NIDB"), v("HMb"), False, False)
        payload(2816, 4096)
        iota(v("BIG", 0, 4096), [[0, 4096]], 0, 0)
        ts(v("HME", 0, 257), v("b7", 0, 257), 8192.0, OP.is_ge)
        tt(v("T4"), v("TWE"), v("HME", 1, 257), OP.mult)
        tt(v("T4"), v("T4"), v("HK"), OP.max)

        def maxscan(out, src, rc, ini, fillers):
            red(v("RC", rc, rc + 1), src, OP.max)
            tr(v("b6", 128, 256, 1, ONEROW), v("RC", rc, rc + 1), v("ID"))
            fillers[0]()
            scan(v("ROW", 1, 129, 1, ONEROW), v("ROW2", 0, 128, 1, ONEROW), v("b6", 128, 256, 1, ONEROW), 0.0, OP.max, OP.max)
            mm(v("b6", ini, ini + 1), v("ROW", 0, 128, 1, ONEROW), v("ID", 0, 1, 1, ONEROW), True, True)
            fillers[1]()
            scan(out, src, src, v("b6", ini, ini + 1), OP.max, OP.max)

        def f1():
            ts(v("HEC"), v("HME", 0, 256), -8192.0, OP.mult)

        def f2():
            tt(v("HEC"), v("HEC"), v("b7", 0, 256), OP.add)
        maxscan(v("RS", 1, 257), v("T4"), 1, 4, (f1, f2))
        tt(v("KI"), v("RS", 1, 257), v("b2", 0, 256), OP.is_gt)
        red(v("RC", 2, 3), v("KI"), OP.add)
        mm(v("b6", 6, 7), v("ID"), GB2, True, False)
        mm(v("b6", 6, 7), v("TRI2"), v("RC", 2, 3), False, True)
        copy(v("RS", 0, 1), v("b6", 4, 5))
        tt(v("OX"), v("RS", 0, 256), v("VG"), OP.is_le)
        scan(v("J2", 1, 257), v("KI"), v("KI"), v("b6", 6, 7), OP.add, OP.add)
        copy(v("J2", 0, 1), v("b6", 6, 7))
        act(v("J0"), v("J2", 1, 257), ACT.Copy)
        rows("GH", 3, 16, "J0")
        tt(v("T5"), v("J2", 0, 256), v("OX"), OP.mult)

        def f3():
            tt(v("J1"), v("J2", 1, 257), v("J0"), OP.subtract)
            rows("GH", 4, 16, "J1")

        def f4():
            ts(v("OUT"), v("KI"), -1.0, OP.mult, 1.0, OP.add)
        maxscan(v("T6"), v("T5"), 3, 8, (f3, f4))
        tt(v("POS"), v("b0", 0, 256), v("T6"), OP.add)
        copy(v("OFF"), v("POS"))
        act(v("P0"), v("POS"), ACT.Copy)
        rows("GV", 0, 0, "P0")
        mm(v("b1", 0, 256), v("IDB"), v("J0"), True, False)
        mm(v("b1", 0, 256), v("IDB"), v("J1"), False, False)
        mm(v("b1", 0, 256), v("NID"), v("T6"), False, True)
        act(v("S20"), v("b1", 0, 256), ACT.Copy)
        rows("GV", 2, 0, "S20")
        tt(v("P1"), v("POS"), v("P0"), OP.subtract)
        rows("GV", 1, 0, "P1")
        copy(ind(v("BIG", 0, 20480), v("OFF", 0, 192)), v("VPAY", 0, 3072))
        mm(v("b3", 0, 256), v("NID"), v("HEC"), False, True)
        mm(v("b5", 0, 256), v("NID"), v("J2", 0, 256), True, False)
        for k in range(4):
            act(v("G1", 1024 * k, 1024 * k + 1024), ind(v("GH", 16, 4112), v("EL", 64 * k, 64 * k + 64)), ACT.Copy)
            bwd(v("b5", 64 * k, 64 * k + 64), "L2", "G1", 1024 * k, 64, False, k == 3)
        tt(v("S21"), v("b1", 0, 256), v("S20"), OP.subtract)
        rows("GV", 3, 0, "S21")
        tt(v("T5"), v("OUT"), v("b5", 0, 256), OP.mult)
        tt(v("T5"), v("T5"), v("b3", 0, 256), OP.add)
        act(v("Z0"), v("T5"), ACT.Copy)
        rows("GV", 4, 0, "Z0")
        tt(v("Z1"), v("T5"), v("Z0"), OP.subtract)
        rows("GV", 5, 0, "Z1")
        copy(ind(v("BIG", 0, 20480), v("OFF", 192, 256)), v("VPAY", 3072, 4096))
        for k in range(4):
            a = 1024 * k
            scan(v("VLS", a, a + 1024), v("BIG", a, a + 1024), v("BIG", a, a + 1024), 0.0 if k == 0 else v("VLS", a - 1, a), OP.max, OP.max)
            bwd(v("b%d" % k, 0, 64), "LP", "VLS", a, 64)
            if k == 2:
                ts(v("VLL", 0, 64), v("b0", 0, 64), -1.0, OP.add)
        for k in range(1, 3):
            ts(v("VLL", 64 * k, 64 * k + 64), v("b%d" % k, 0, 64), -1.0, OP.add)

        def gat(k, out, win):
            i = ind(win, v("VLL", 64 * k, 64 * k + 64))
            if k < 2:
                act(out, i, ACT.Copy)
            else:
                copy(out, i)
        for k in (0, 2, 1, 3):
            a = 1024 * k
            if k == 3:
                ts(v("VLL", 192, 256), v("b3", 0, 64), -1.0, OP.add)
            gat(k, bg(12288 + a, 12288 + a + 1024), v("GV"))
            bwd(v("b4", 64 * k, 64 * k + 64), "L3", "BIG", BO + 12288 + a, 64)
        for k in (0, 2, 1, 3):
            gat(k, bg(1024 * k, 1024 * k + 1024), v(X))
        act(bg(4096, 6144), bg(0, 2048), ACT.Relu, -1.0)
        act(bg(6144, 8192), bg(2048, 4096), ACT.Relu, -1.0)
        copy(v("PKI"), v("b4", 0, 256))
        ts(v("PPI"), v("PKI"), 12, OP.arith_shift_right)
        ts(v("PSI"), v("PKI"), 4095, OP.bitwise_and)
        tt(v("T1"), v("QW"), v("PPI"), OP.subtract)
        tt(v("T2"), v("T1"), v("PSI"), OP.is_gt)
        ts(v("T3"), v("T1"), 0.0, OP.is_gt)
        tt(v("T3"), v("T3"), v("T2"), OP.add)
        tt(v("T4"), v("T3"), v("PSI"), OP.mult)
        tt(v("T4"), v("QW"), v("T4"), OP.subtract)
        copy(v("QL"), v("T4"))
        dst = T.cores[(rank + 1) % len(T.cores)]
        src = T.cores[(rank - 1) % len(T.cores)]

        def send(name, to, rsem, lsem):
            rid, pid, _se = topo.addr(dst)
            add("G", [v(name)], [], lambda: g.remote_dma(ap(to), ap(v(name)), T.sem[rsem], T.sem[lsem], pid, rid, topo.mask(core, dst)),
                lsem, len(topo.engines(core, dst)))
            add("R", [], [to], None, rsem, len(topo.engines(src, core)))

        def sizes(out, lo, hi, onv):
            i = ind(bg(12288, 16384), v("QL", lo // 16, hi // 16))
            if onv:
                copy(out, i)
            else:
                act(out, i, ACT.Copy)

        def szc(i):
            s = v("SZB", 256 * i, 256 * i + 256) if i < 14 else v("LZ%d" % t, 256 * (i - 14), 256 * (i - 14) + 256)
            mm(v("b7", 0, 256), v("L4", 128 * i, 128 * i + 128), s, i == 0, i == 15)

        def xl(lo, hi):
            return ind(bg(0, 12288), v("XL", lo // 16, hi // 16))
        sizes(v("SZS"), 3584, 4096, False)
        send("SZS", v("LZ%d" % t), "rz%d" % t, "lz%d" % t)
        for k in (0, 3, 1, 4, 2, 5, 6):
            sizes(v("SZB", 512 * k, 512 * k + 512), 512 * k, 512 * k + 512, k < 3)
            szc(2 * k)
            szc(2 * k + 1)
            if k == 0:
                ts(v("T3"), v("T3"), 4096.0, OP.mult)
                tt(v("T5"), v("T3"), v("T4"), OP.add)
                copy(v("XL"), v("T5"))
        szc(14)
        szc(15)
        ts(bg(8192, 12288), bg(0, 4096), 2.0, OP.subtract, 0.0, OP.max)
        act(v("XS"), xl(3584, 4096), ACT.Copy)
        send("XS", v(XN, 3584, 4096), "rx%d" % t, "lx%d" % t)
        if t < RO - 1:
            act(v(XN, 1024, 3584), xl(1024, 3584), ACT.Copy)
            tt(SZ, v("b7", 0, 256), v("REM"), OP.min)
            tables()
            copy(v(XN, 0, 1024), xl(0, 1024))
        else:
            copy(v(XN, 0, 1024), xl(0, 1024))
            dma(v("y", 0, 1024), v(XN, 0, 1024))
            act(v(XN, 2048, 3584), xl(2048, 3584), ACT.Copy)
            copy(v(XN, 1024, 2048), xl(1024, 2048))
            dma(v("y", 1024, 2048), v(XN, 1024, 2048))
            tt(SZ, v("b7", 0, 256), v("REM"), OP.min)
            tt(v("T1"), v("VC"), SZ, OP.add)
            dma(v("y", 2048, 3584), v(XN, 2048, 3584))
            dma(v("ye", 0, 4096, 1, (0, 8, 1)), v("T1"))
            dma(v("y", 3584, 4096), v(XN, 3584, 4096))

    qidx = {}
    hist = {}
    known = {}
    need = set()
    for k, o in enumerate(ops):
        q = o["q"]
        o["k"] = k
        if o["sem"] is None:
            o["tok"] = (q, qidx.get(q, 0))
            qidx[q] = qidx.get(q, 0) + 1
        else:
            o["tok"] = ("*" + o["sem"], 0)
        deps = []
        for wr, lst in ((0, o["r"]), (1, o["w"])):
            for x in lst:
                name = x[0]
                psum = name[0] == "b" and len(name) == 2
                m = pm(x[1])
                keep = []
                for h in hist.get(name, []):
                    ho, hw, hx = h
                    over = (pm(hx[1]) & m) and hx[2] < x[3] and x[2] < hx[3]
                    same = ho["q"] == q and o["sem"] is None and ho["sem"] is None
                    if psum and not same:
                        deps.append(ho)
                    elif psum and q == "P":
                        pass
                    elif over and (wr or hw):
                        deps.append(ho)
                    if wr and not psum and hx[2] >= x[2] and hx[3] <= x[3] and (pm(hx[1]) & ~m) == 0 and x[4] == 1:
                        continue
                    keep.append(h)
                if psum and len(keep) > 200:
                    keep = keep[-200:]
                hist[name] = keep
        kn = known.setdefault(q if q != "R" else ("R", k), {})
        waits = []
        best = {}
        for ho in deps:
            tq, ti = ho["tok"]
            if tq not in best or best[tq]["tok"][1] < ti:
                best[tq] = ho
        for ho in sorted(best.values(), key=lambda z: -z["k"]):
            tq, ti = ho["tok"]
            if kn.get(tq, -1) >= ti:
                continue
            waits.append(ho)
            need.add(ho["tok"])
            for a, b in ho["kn"].items():
                if kn.get(a, -1) < b:
                    kn[a] = b
            kn[tq] = max(kn.get(tq, -1), ti)
        o["waits"] = waits
        o["kn"] = dict(kn)
        for wr, lst in ((0, o["r"]), (1, o["w"])):
            for x in lst:
                hist.setdefault(x[0], []).append((o, wr, x))
    cnt = {}
    eng_of = {"V": g.vector, "S": g.scalar, "P": g.tensor, "G": g, "Y": g.sync}
    sem_of = {"V": "sV", "S": "sS", "P": "sP", "G": "sG"}
    for o in ops:
        q = o["q"]
        if q == "R":
            o["val"] = o["n"]
            continue
        e = eng_of[q]
        for ho in o["waits"]:
            e.wait_ge(T.sem[ho["sem"] or sem_of[ho["q"]]], ho["val"])
        r = o["call"]()
        if o["sem"] is not None:
            o["val"] = o["n"]
            if q != "G":
                r.then_inc(T.sem[o["sem"]], o["n"])
        elif o["tok"] in need:
            cnt[q] = cnt.get(q, 0) + 1
            o["val"] = cnt[q]
            r.then_inc(T.sem[sem_of[q]], 1)
    for q in ("V", "S", "P", "G"):
        if cnt.get(q, 0):
            g.wait_ge(T.sem[sem_of[q]], cnt[q])
    for o in ops:
        if o["sem"] is not None:
            g.wait_ge(T.sem[o["sem"]], o["n"])
